import numpy as np, ml_dtypes
CORES = [83,85,87,115,117,119]
N = 6
BF = ml_dtypes.bfloat16
def gentries(a):
    return np.ascontiguousarray(a.reshape(8, 16, -1).transpose(0, 2, 1)).reshape(8, -1)
def gtable(e):
    e = np.asarray(e); return np.ascontiguousarray(e.reshape(8, -1, 16).transpose(0, 2, 1)).reshape(128, -1).astype(np.int32)
W, n, V, C, Z = 5, 2048, 16384, 512, 128
def counts(rng, h, z):
    c = np.zeros((N, 8, W), np.int64)
    for r in range(N):
        for g in range(8):
            m = int(h[r, g] - z[r, g]) - (W - 2); b = np.sort(rng.integers(0, m + 1, W - 3))
            c[r, g, 0] = n - h[r, g]; c[r, g, 1:W - 1] = np.diff(np.concatenate([[0], b, [m]])) + 1; c[r, g, W - 1] = z[r, g]
    return c
def some(rng):
    return rng.integers(C - C // 4, C + 1, (N, 8)), rng.integers(Z // 2, Z + 1, (N, 8))
def names(rng):
    return np.stack([np.stack([rng.permutation(V)[:n] for g in range(8)]) for r in range(N)]).astype(np.int64)
def depths(rng, c):
    return np.stack([np.stack([rng.permutation(np.repeat(np.arange(W), c[r, g])) for g in range(8)]) for r in range(N)])
def link(rng, o, dep):
    x = np.zeros((N, 8, n), np.int64)
    for r in range(N):
        q = (r + 1) % N
        for g in range(8):
            m = np.ones(V, bool); m[o[q, g]] = False; free = np.flatnonzero(m)
            v = free[rng.integers(0, len(free), n)]
            for k in range(1, W):
                i = np.flatnonzero(dep[r, g] == k)
                if len(i):
                    t = np.flatnonzero(dep[q, g] == k - 1 if k < W - 1 else dep[q, g] >= W - 2)
                    v[i] = o[q, g][t[rng.integers(0, len(t), len(i))]]
            x[r, g] = v
    return x
def pack(o, x, s):
    return {"own": np.stack([gtable(a) for a in o]), "nxt": np.stack([gtable(a) for a in x]), "pts": np.asarray(s).astype(np.int32)}
def points(rng):
    return rng.integers(0, 256, (N, 8, n))
def setup_inputs(rng):
    h, z = some(rng); o = names(rng); dep = depths(rng, counts(rng, h, z))
    return pack(o, link(rng, o, dep), points(rng))
def setup_inputs_full(rng):
    o = names(rng); c = counts(rng, np.full((N, 8), C), np.full((N, 8), Z)); e = rng.permutation(8)[:4]
    c[:, e, 1:W - 2] = 1; c[:, e, W - 2] = C - Z - (W - 3)
    dep = depths(rng, c)
    return pack(o, link(rng, o, dep), points(rng))
def setup_inputs_few(rng):
    h, z = some(rng); e = rng.permutation(8); q = int(rng.integers(0, N)); o = names(rng)
    z[:, e[2]] = 1; z[:, e[3]] = np.where(rng.random(N) < 0.5, 0, z[:, e[3]]); z[q, e[3]] = 0; z[:, e[4]] = Z; h[:, e[4]] = C
    c = counts(rng, h, z); c[:, e[0], 0] = n; c[:, e[0], 1:] = 0
    for t in range(W - 1):
        r = (q - t) % N; c[r, e[1], 0] += np.sum(c[r, e[1], t + 1:]); c[r, e[1], t + 1:] = 0
    dep = depths(rng, c)
    return pack(o, link(rng, o, dep), points(rng))
def setup_inputs_repeats(rng):
    h, z = some(rng); o = names(rng); dep = depths(rng, counts(rng, h, z)); x = link(rng, o, dep)
    for r in range(N):
        for g in range(8):
            for k in (0, W - 1):
                i = np.flatnonzero(dep[r, g] == k); x[r, g, i] = x[r, g, i[0]]
    return pack(o, x, points(rng))
def setup_inputs_ends(rng):
    h, z = some(rng); dep = depths(rng, counts(rng, h, z))
    o = 1 + np.stack([np.stack([rng.permutation(V - 2)[:n] for g in range(8)]) for r in range(N)]).astype(np.int64)
    for r in range(N):
        for g in range(0, 8, 2):
            o[r, g, 0] = 0; o[r, g, n - 1] = V - 1; a = dep[r, g]
            i = np.flatnonzero(a == W - 1); j = i[rng.integers(0, len(i))]; u, v = int(a[0]), int(a[j]); a[j] = u; a[0] = v
            i = np.flatnonzero(a[1:] == W - 1) + 1; j = i[rng.integers(0, len(i))]; u, v = int(a[n - 1]), int(a[j]); a[j] = u; a[n - 1] = v
    x = link(rng, o, dep)
    x[:, 0::2, 0] = V - 1; x[:, 0::2, n - 1] = 0
    for g in range(1, 8, 2):
        m = (dep[:, g] == 0) & (rng.random((N, n)) < 0.5)
        x[:, g] = np.where(m, rng.integers(0, 2, (N, n)) * (V - 1), x[:, g])
    return pack(o, x, 255 * rng.integers(0, 2, (N, 8, n)))
def setup_inputs_spread(rng):
    z = np.maximum(Z >> rng.integers(0, 7, (N, 8)), 1); h = z + np.maximum((C - Z) >> rng.integers(0, 7, (N, 8)), W - 2)
    o = np.stack([np.stack([(rng.integers(0, V) + rng.permutation(n + n // 8)[:n]) % V for g in range(8)]) for r in range(N)]).astype(np.int64)
    o[:, 1::2] = np.sort(o[:, 1::2], axis=2)
    dep = depths(rng, counts(rng, h, z))
    return pack(o, link(rng, o, dep), 255 >> rng.integers(0, 9, (N, 8, n)))
def followers(o, x):
    to = np.zeros((N, 8, n), np.int64)
    for r in range(N):
        for g in range(8):
            where = np.full(V, -1, np.int64); where[o[(r + 1) % N, g]] = np.arange(n); to[r, g] = where[x[r, g]]
    return to
def step(p, v, t):
    return np.take_along_axis(np.roll(v, -t, axis=0), p, axis=2)
def chains(to, s):
    p = np.broadcast_to(np.arange(n), (N, 8, n)); tot = s.astype(np.int64)
    for t in range(1, W):
        p = np.where(p >= 0, step(np.maximum(p, 0), to, t - 1), -1)
        tot = tot + np.where(p >= 0, step(np.maximum(p, 0), s, t), 0)
    return p, tot
def check_inputs(d):
    try:
        o = np.stack([gentries(a) for a in d["own"]]).astype(np.int64); x = np.stack([gentries(a) for a in d["nxt"]]).astype(np.int64); s = np.asarray(d["pts"]).astype(np.int64)
        if o.shape != (N, 8, n) or x.shape != (N, 8, n) or s.shape != (N, 8, n): return ["shapes"]
        bad = []
        if s.min() < 0 or s.max() > 255: bad.append("points")
        if o.min() < 0 or o.max() >= V or x.min() < 0 or x.max() >= V: return bad + ["names in range"]
        if (np.diff(np.sort(o, axis=2), axis=2) == 0).any(): return bad + ["own names differ"]
        to = followers(o, x); p, tot = chains(to, s)
        if np.max(np.count_nonzero(to >= 0, axis=2)) > C: bad.append("followers")
        if np.max(np.count_nonzero(p >= 0, axis=2)) > Z: bad.append("kept")
        return bad
    except Exception:
        return ["shapes"]
def reference(own, nxt, pts):
    o = np.stack([gentries(a) for a in own]).astype(np.int64); x = np.stack([gentries(a) for a in nxt]).astype(np.int64)
    p, tot = chains(followers(o, x), pts)
    yk = np.full((N, 8, Z), -1, np.float32); ys = np.zeros((N, 8, Z), np.float32)
    for r in range(N):
        for g in range(8):
            i = np.flatnonzero(p[r, g] >= 0)
            yk[r, g, :len(i)] = o[r, g, i]; ys[r, g, :len(i)] = tot[r, g, i]
    return {"yk": yk, "ys": ys}

@@ -1,0 +1,313 @@
+from concourse.bass import DstId, RemoteDMATransfer
+from concourse.mybir import dt, AluOpType, AxisListType, ActivationFunctionType
+
+A = AluOpType
+F = ActivationFunctionType
+NV = 16384
+NE = 2048
+FILLV = 128.0
+NONE = 16 * 128 + 128
+DW = NONE + 8
+BIG = 8192.0
+HUGE = 65536.0
+CC = 512
+ZZ = 128
+NVEC = 8192
+NDMA = 4096
+
+
+def _bufs():
+    d = {}
+    for where, typ, items in (
+            ("sbuf", "int32", "owni:128 nxti:128 ptsi:128 ownr:128 oi:128 pi:1 pm:1"),
+            ("sbuf", "uint16", "ou:128 nu:128 fu:128 fl1:128 fl2:128 fl3:128 du:128 pu:32 du2:32"),
+            ("sbuf", "bfloat16", "ptsb:128 ptl1:128 ptl2:128 ptl3:128 ptl4:128 ptr1:2048 ptr2:2048 ptr3:2048 ptr4:2048 p1:2048 p2:2048 p3:2048"
+                                 " tab:16384 val:2048 gat:2048 cb:512 ones:512 zb:128 hi:256 lo:256 t1:256 t2:256 bas:256"
+                                 " bd0:128 bd:128 tri:128 upp:128 idb:128 l4:128 eg:8 ww:2048 ka:128 kb2:512 kb3:512 vb:129 vb2:33"),
+            ("sbuf", "float32", "w4:%d d3:%d d2:%d d1:%d ownf:128 ptf:128 tf:128 np:2048 xx:2048 cwin:2560 s1:512 sw:512 rr:512 owin:640 of:128"
+                                " zf:128 pmf:1 c0:1 c1:1 c3:1 co:1 cc:1 wc:1 n1:1 i8:8 bcol:8 idf:128 onef:128 hm:512 ii:128 i512:128 i128:32"
+                                " nv:128 iv:128 xs:128 ds:128 nv2:32 iv2:32 xs2:32 ds2:32" % (DW, DW, DW, DW)),
+            ("psum", "float32", "pspa:1024 pspb:1024 psf0:512 psf1:512 psd:512 psw:512")):
+        for it in items.split():
+            name, w = it.split(":")
+            d[name] = (where, [128, int(w)], typ)
+    return d
+
+
+SCRATCH = _bufs()
+EV = """ones tab0 tabv tabs pi pm pmf c0 c1 c3 cc co n1 wc hl t1 t2 bas i8 bcol val onef bd0 bd tri upp idb idf l4 zb zf
+kab ii i512 i128 w4t tails cpre vz opre opre2 np0 ww0 eg ww ownf ptf tr tf psk4 w4 ptsb nu ou scat ga gb fa fb fuv vb nv iv dl xs ds du
+xa xb xx0 xx1 cs0 cs cb pw pu rh hm hmv d3 d2 d1 s1 rr sw vb2 nv2 iv2 dl2 xs2 ds2 du2 osc oi of""".split()
+SEMAPHORES = ["e_" + e for e in EV] + ["ldo", "ldn", "ldp", "dfl", "dnp", "dp4", "dp3", "dp2", "dp1", "rep3", "rep2", "rep1", "oarr", "osent", "parr", "psent",
+                                       "fa1", "fa2", "fa3", "fs1", "fs2", "fs3", "out1", "out2"]
+
+
+def rank_program(g, core, T, topo):
+    rank = T.rank_of(core)
+    if rank is None:
+        return
+    n = len(T.cores)
+    V, S, P, Y = g.vector, g.scalar, g.tensor, g.sync
+    back = [T.cores[(rank - k) % n] for k in range(n)]
+
+    def sem(e):
+        return T.sem["e_" + e]
+
+    def done(ins, e):
+        ins.then_inc(sem(e), 1)
+
+    def wait(q, *es):
+        for e in es:
+            if isinstance(e, tuple):
+                q.wait_ge(sem(e[0]), e[1])
+            else:
+                q.wait_ge(sem(e), 1)
+
+    def const(buf, v, e):
+        done(g.iota(buf, [[0, buf.shape[1]]], int(v), 0, allow_small_or_imprecise_dtypes=True), e)
+
+    es = set(topo.engines(core, back[1]))
+    for k in range(2, n - 1):
+        es &= set(topo.engines(core, back[k]))
+    E = sorted(es)[0:8:2]
+    M = sum(1 << e for e in E)
+    NEG = len(E)
+
+    def send(buf_out, buf_in, dst, rs, ls):
+        rid, pid = topo.addr(dst)[:2]
+        g.remote_dma(buf_out[:], buf_in[:], T.sem[rs], T.sem[ls], pid, rid, M)
+
+    Y.dma_start(T.owni[:], T.own[:]).then_inc(T.sem.ldo, 16)
+    Y.dma_start(T.ptsi[:], T.pts[:]).then_inc(T.sem.ldp, 16)
+    S.dma_start(T.nxti[:], T.nxt[:]).then_inc(T.sem.ldn, 16)
+
+    done(g.iota(T.pi[:], [[0, 1]], 0, 1), "pi")
+    done(g.iota(T.i8[:], [[16, 8]], 0, 0, allow_small_or_imprecise_dtypes=True), "i8")
+    done(g.iota(T.hi[:], [[1, 16], [0, 16]], 0, 0, allow_small_or_imprecise_dtypes=True), "hl")
+    done(g.iota(T.lo[:], [[0, 16], [1, 16]], 0, 0, allow_small_or_imprecise_dtypes=True), "hl")
+    g.wait_ge(T.sem.ldo, 16)
+    send(T.ownr, T.owni, back[1], "oarr", "osent")
+    wait(g, "ones")
+    done(g.affine_select(T.bd0[:], T.ones[:, 0:128], [[-16, 8], [0, 16]], A.is_ge, 0.0, 0, 1), "bd0")
+    wait(g, "bd0")
+    done(g.affine_select(T.bd[:], T.bd0[:], [[16, 8], [0, 16]], A.is_ge, 0.0, 15, -1), "bd")
+    wait(g, "ptsb")
+    ids, dsts = [], []
+    for k in (4, 3, 2, 1):
+        rid, pid = topo.addr(back[k])[:2]
+        ids.append(DstId(rid=rid, pnc=pid))
+        dsts.append(T["ptl%d" % k][:])
+    g.remote_dma_fused([RemoteDMATransfer(dst_ids=ids, dma_engine_mask=M, remote_sem=T.sem.parr, src=T.ptsb[:], dsts=dsts)], local_sem=T.sem.psent)
+    const(T.onef[:], 1, "onef")
+    wait(g, "onef")
+    done(g.affine_select(T.idf[:], T.onef[:], [[-1, 128]], A.is_equal, 0.0, 0, 1), "idf")
+    const(T.ww[:], 0, "ww0")
+    done(g.affine_select(T.l4[0:8, :], T.ones[0:8, 0:128], [[-1, 8], [0, 16]], A.is_equal, 0.0, 0, 1), "l4")
+    done(g.affine_select(T.idb[:], T.ones[:, 0:128], [[-1, 128]], A.is_equal, 0.0, 0, 1), "idb")
+    wait(g, "bd")
+    done(g.affine_select(T.tri[:], T.bd[:], [[1, 128]], A.is_gt, 0.0, 0, -1), "tri")
+    done(g.affine_select(T.upp[:], T.bd[:], [[-1, 128]], A.is_ge, 0.0, 0, 1), "upp")
+    done(g.iota(T.ii[:], [[16, 128]], CC, 0, allow_small_or_imprecise_dtypes=True), "ii")
+    const(T.zf[:], 0, "zf")
+    const(T.vb[:, 0:1], 0, "vz")
+    const(T.vb2[:, 0:1], 0, "vz")
+    const(T.w4[:, NE:DW], -BIG, "w4t")
+    wait(g, ("fuv", 2))
+    send(T.fl3, T.fu, back[3], "fa3", "fs3")
+    send(T.fl2, T.fu, back[2], "fa2", "fs2")
+    send(T.fl1, T.fu, back[1], "fa1", "fs1")
+    for b in ("d3", "d2", "d1"):
+        const(T[b][:, NE:DW], -BIG, "tails")
+    const(T.zb[:], 0, "zb")
+    wait(g, "zb")
+    done(g.affine_select(T.ka[0:16, :], T.zb[0:16, :], [[0, 8], [1, 16]], A.not_equal, HUGE, 0, -1), "kab")
+    done(g.affine_select(T.kb3[0:16, :], T.ones[0:16, :], [[0, 32], [1, 16]], A.not_equal, 0.0, 0, -1), "kab")
+    done(g.affine_select(T.kb2[0:16, :], T.ones[0:16, :], [[0, 32], [1, 16]], A.is_equal, -1.0, 0, -1), "kab")
+    const(T.owin[:, 0:ZZ], 32, "opre")
+
+    wait(Y, "tab0")
+    for a in range(NVEC, NVEC + NDMA, 2048):
+        Y.dma_start(T.tab[:, a:a + 2048], T.tab[:, 0:2048]).then_inc(T.sem.dfl, 16)
+    Y.wait_ge(T.sem.parr, 4 * NEG)
+    for k in (4, 3, 2, 1):
+        Y.dma_start(T["ptr%d" % k][0:8, :], T["ptl%d" % k][:]).then_inc(T.sem["dp%d" % k], 16)
+    wait(Y, "ptf", ("np0", 4))
+    Y.dma_start(T.np[2:128:16, :], T.ptf[:]).then_inc(T.sem.dnp, 16)
+    wait(Y, "tf")
+    for h in range(8):
+        Y.dma_start(T.np[16 * h + 1:16 * h + 2, :], T.tf[:, 16 * h:16 * h + 16]).then_inc(T.sem.dnp, 16)
+    for k in (3, 2, 1):
+        Y.wait_ge(T.sem["dp%d" % k], 16)
+        for s in range(16):
+            Y.dma_start(T["p%d" % k][s:128:16, :], T["ptr%d" % k][0:8, :]).then_inc(T.sem["rep%d" % k], 16)
+
+    done(V.memset(T.ones[:], 1.0), "ones")
+    done(V.memset(T.tab[:, 0:2048], FILLV), "tab0")
+    wait(V, "pi")
+    done(V.tensor_scalar(T.pm[:], T.pi[:], 15, None, A.bitwise_and), "pm")
+    wait(V, "pm")
+    done(V.tensor_copy(T.pmf[:], T.pm[:]), "pmf")
+    done(V.tensor_scalar(T.c0[:], T.pm[:], 0.0, None, A.is_equal), "c0")
+    done(V.tensor_scalar(T.c1[:], T.pm[:], 1.0, None, A.is_equal), "c1")
+    done(V.tensor_scalar(T.c3[:], T.pm[:], 3.0, None, A.is_equal), "c3")
+    done(V.memset(T.tab[:, 2048:4096], FILLV), "tabv")
+    wait(V, "c0", "c1", "c3")
+    done(V.tensor_tensor(T.cc[:], T.c0[:], T.c3[:], A.add), "cc")
+    done(V.tensor_scalar(T.wc[:], T.c0[:], 16.0, T.c3[:], A.mult, A.add), "wc")
+    wait(V, ("hl", 2), "i8", "cc")
+    done(V.tensor_scalar(T.co[:], T.cc[:], -FILLV, FILLV, A.mult, A.add), "co")
+    done(V.tensor_scalar(T.t1[:], T.hi[:], T.c0[:], None, A.mult), "t1")
+    done(V.tensor_scalar(T.t2[:], T.lo[:], T.c3[:], None, A.mult), "t2")
+    V.wait_ge(T.sem.ldp, 16)
+    done(V.tensor_copy(T.ptsb[:], T.ptsi[:]), "ptsb")
+    wait(V, "co", "t1", "t2")
+    done(V.tensor_tensor(T.bas[:], T.t1[:], T.t2[:], A.add), "bas")
+    done(V.tensor_scalar(T.bcol[:], T.i8[:], T.c0[:], T.co[:], A.mult, A.add), "bcol")
+    wait(V, "bas", "bcol")
+    for a in range(8):
+        done(V.tensor_scalar(T.val[:, 256 * a:256 * a + 256], T.bas[:], T.bcol[:, a:a + 1], None, A.add), "val")
+    done(V.memset(T.tab[:, 4096:NVEC], FILLV), "tabv")
+    V.wait_ge(T.sem.ldo, 16)
+    done(V.tensor_scalar(T.ownf[:], T.owni[:], 16.0 + 16.0 - FILLV, None, A.add), "ownf")
+    wait(V, "bd", "wc")
+    done(V.tensor_scalar(T.eg[:], T.bd[:, 0:128:16], T.wc[:], None, A.mult), "eg")
+    V.wait_ge(T.sem.ldn, 16)
+    done(V.tensor_copy(T.nu[:], T.nxti[:]), "nu")
+    done(V.tensor_scalar(T.ptf[:], T.ptsi[:], 16.0 + 16.0 - FILLV, None, A.add), "ptf")
+    done(V.tensor_scalar(T.n1[:], T.c1[:], -1.0, 1.0, A.mult, A.add), "n1")
+    V.wait_ge(T.sem.oarr, NEG)
+    done(V.tensor_copy(T.ou[:], T.ownr[:]), "ou")
+    wait(V, "ou", ("tabv", 2), ("tabs", 2), ("val", 8), "tab0")
+    V.wait_ge(T.sem.dfl, 16 * (NDMA // 2048))
+    done(V.tensor_copy(T.tab[:].indirect(T.ou[:, 0:128]), T.val[:]), "scat")
+    wait(V, "scat", "nu")
+    done(V.tensor_copy(T.gat[:, 0:512], T.tab[:].indirect(T.nu[:, 0:32])), "ga")
+    done(V.tensor_copy(T.gat[:, 1024:1536], T.tab[:].indirect(T.nu[:, 64:96])), "gb")
+
+    wait(S, "tab0")
+    for a in range(NVEC + NDMA, NV, 2048):
+        done(S.activation(T.tab[:, a:a + 2048], T.tab[:, 0:2048], F.Silu), "tabs")
+    wait(S, "ones")
+    for a in range(4):
+        done(S.activation(T.np[:, 512 * a:512 * a + 512], T.ones[:], F.Copy, scale=16.0), "np0")
+    wait(S, "tr")
+    done(S.activation(T.tf[:], T.psd[:, 0:128], F.Copy), "tf")
+    wait(S, "eg", "ww0")
+    for s in range(16):
+        done(S.activation(T.ww[:, 128 * s + s:128 * s + 128:16], T.eg[:], F.Copy), "ww")
+    done(S.activation(T.cwin[:, 0:CC], T.ones[:], F.Copy, scale=FILLV + 16.0), "cpre")
+    wait(S, ("psk4", 4))
+    done(S.activation(T.w4[:, 0:1024], T.pspa[:], F.Copy), "w4")
+    done(S.activation(T.w4[:, 1024:2048], T.pspb[:], F.Copy), "w4")
+    wait(S, "scat", "nu")
+    done(S.activation(T.gat[:, 512:1024], T.tab[:].indirect(T.nu[:, 32:64]), F.Copy), "ga")
+    done(S.activation(T.gat[:, 1536:2048], T.tab[:].indirect(T.nu[:, 96:128]), F.Copy), "gb")
+    wait(S, "du", "xx0", "cpre")
+    done(S.activation(T.cwin[:].indirect(T.du[:, 0:64]), T.xx[:, 0:1024], F.Silu), "cs0")
+    wait(S, "cs0", "xx1")
+    done(S.activation(T.cwin[:].indirect(T.du[:, 64:128]), T.xx[:, 1024:2048], F.Silu), "cs")
+    wait(S, "cs")
+    done(S.activation(T.cb[:], T.cwin[:, 0:CC], F.Copy), "cb")
+    wait(S, "hm")
+    done(S.activation(T.hm[:], T.psf1[:], F.Copy), "hmv")
+    wait(S, "pu", "d1", ("tails", 3), "n1")
+    done(S.activation(T.rr[:], T.d1[:].indirect(T.pu[:, 0:32]), F.Identity, scale=T.n1[:]), "rr")
+
+    wait(P, "ownf", "idf")
+    done(P.transpose(T.psd[:, 0:128], T.ownf[:], T.idf[:]), "tr")
+    P.wait_ge(T.sem.dp4, 16)
+    wait(P, "l4")
+    for b in range(4):
+        ps = (T.pspa, T.pspb)[b // 2]
+        done(P.matmul(ps[:, 512 * (b % 2):512 * (b % 2) + 512], T.l4[0:8, :], T.ptr4[0:8, 512 * b:512 * b + 512], True, True), "psk4")
+    for c, (ps, e, e2) in enumerate(((T.psf0, "fa", "ga"), (T.psf1, "fb", "gb"))):
+        wait(P, ("ww", 16), (e2, 2))
+        for s in range(16):
+            m = P.matmul(ps[:, 0:64], T.ww[:, 128 * s:128 * s + 128], T.gat[:, 1024 * c + s:1024 * c + 1024:16], s == 0, s == 15)
+        done(m, e)
+    wait(P, ("w4", 2), "idb")
+    for b in range(2):
+        done(P.matmul(T.pspa[:, 512 * b:512 * b + 512], T.idb[:], T.gat[:, 512 * b:512 * b + 512], True, True), "xa")
+    wait(P, "tri", "upp", ("vb", 2), ("vz", 2), "tf")
+    P.matmul(T.psd[:, 0:128], T.tri[:], T.vb[:, 1:129], True, False)
+    done(P.matmul(T.psd[:, 0:128], T.upp[:], T.vb[:, 0:128], False, True), "dl")
+    for b in range(2):
+        done(P.matmul(T.pspb[:, 512 * b:512 * b + 512], T.idb[:], T.gat[:, 1024 + 512 * b:1536 + 512 * b], True, True), "xb")
+    wait(P, ("kab", 3), ("fuv", 2), ("vb", 2), ("nv", 2))
+    done(P.matmul(T.psf1[:], T.ka[0:16, :], T.kb3[0:16, :], True, True), "hm")
+    done(P.matmul(T.psf0[:], T.ka[0:16, :], T.kb2[0:16, :], True, True), "rh")
+    wait(P, "cb")
+    for s in range(16):
+        m = P.matmul(T.psw[:, 0:32], T.ww[:, 128 * s:128 * s + 128], T.cb[:, s:CC:16], s == 0, s == 15)
+    done(m, "pw")
+    wait(P, "vb2", "xs")
+    P.matmul(T.psd[:, 0:32], T.tri[:], T.vb2[:, 1:33], True, False)
+    done(P.matmul(T.psd[:, 0:32], T.upp[:], T.vb2[:, 0:32], False, True), "dl2")
+
+    wait(V, "ii", "pmf")
+    done(V.tensor_scalar(T.i512[:], T.ii[:], T.pmf[:], None, A.add), "i512")
+    done(V.tensor_scalar(T.i128[:], T.ii[:, 0:32], T.pmf[:], float(ZZ - CC), A.add, A.add), "i128")
+    for c, (ps, e) in enumerate(((T.psf0, "fa"), (T.psf1, "fb"))):
+        wait(V, e)
+        done(V.tensor_copy(T.fu[:, 64 * c:64 * c + 64], ps[:, 0:64]), "fuv")
+        done(V.tensor_scalar(T.vb[:, 1 + 64 * c:65 + 64 * c], ps[:, 0:64], float(NE), None, A.is_lt), "vb")
+        done(V.tensor_scalar(T.nv[:, 64 * c:64 * c + 64], ps[:, 0:64], float(NE), None, A.is_ge), "nv")
+    wait(V, ("nv", 2), "i512")
+    done(V.tensor_tensor(T.iv[:], T.nv[:], T.i512[:], A.mult), "iv")
+    V.wait_ge(T.sem.dnp, 16 * 9)
+    wait(V, ("xa", 2))
+    done(V.tensor_tensor(T.xx[:, 0:1024], T.pspa[:], T.np[:, 0:1024], A.add), "xx0")
+    wait(V, "dl", "zf")
+    done(V.tensor_tensor_scan(T.xs[:], T.psd[:, 0:128], T.zf[:], 0.0, A.add, A.add), "xs")
+    wait(V, "xs", "iv")
+    done(V.tensor_tensor(T.ds[:], T.xs[:], T.iv[:], A.max), "ds")
+    wait(V, "ds")
+    done(V.tensor_copy(T.du[:], T.ds[:]), "du")
+    wait(V, ("xb", 2))
+    done(V.tensor_tensor(T.xx[:, 1024:2048], T.pspb[:], T.np[:, 1024:2048], A.add), "xx1")
+    V.wait_ge(T.sem.fa3, NEG)
+    V.wait_ge(T.sem.rep3, 256)
+    wait(V, ("w4", 2), "w4t")
+    done(V.tensor_tensor(T.d3[:, 0:NE], T.w4[:].indirect(T.fl3[:, 0:128]), T.p3[:], A.add), "d3")
+    V.wait_ge(T.sem.fa2, NEG)
+    V.wait_ge(T.sem.rep2, 256)
+    wait(V, ("tails", 3), "d3")
+    done(V.tensor_tensor(T.d2[:, 0:NE], T.d3[:].indirect(T.fl2[:, 0:128]), T.p2[:], A.add), "d2")
+    V.wait_ge(T.sem.fa1, NEG)
+    V.wait_ge(T.sem.rep1, 256)
+    wait(V, "d2")
+    done(V.tensor_tensor(T.d1[:, 0:NE], T.d2[:].indirect(T.fl1[:, 0:128]), T.p1[:], A.add), "d1")
+    wait(V, "pw")
+    done(V.tensor_scalar(T.pu[:], T.psw[:, 0:32], -272.0, None, A.add), "pu")
+    wait(V, "pu", "d1", "hmv")
+    done(V.tensor_tensor(T.s1[:], T.d1[:].indirect(T.pu[:, 0:32]), T.hm[:], A.add), "s1")
+    wait(V, "s1", "rh")
+    done(V.tensor_tensor_scan(T.sw[:], T.psf0[:], T.s1[:], 0.0, A.max, A.min), "sw")
+    wait(V, "sw")
+    done(V.tensor_scalar(T.vb2[:, 1:33], T.sw[:, 15:CC:16], 0.0, None, A.is_ge), "vb2")
+    done(V.tensor_scalar(T.nv2[:], T.sw[:, 15:CC:16], 0.0, None, A.is_lt), "nv2")
+    wait(V, "nv2", "i128")
+    done(V.tensor_tensor(T.iv2[:], T.nv2[:], T.i128[:], A.mult), "iv2")
+    wait(V, "opre")
+    done(V.tensor_scalar(T.owin[:, 0:ZZ], T.owin[:, 0:ZZ], T.c1[:], None, A.subtract), "opre2")
+    wait(V, "dl2")
+    done(V.tensor_tensor_scan(T.xs2[:], T.psd[:, 0:32], T.zf[:, 0:32], 0.0, A.add, A.add), "xs2")
+    wait(V, "xs2", "iv2")
+    done(V.tensor_tensor(T.ds2[:], T.xs2[:], T.iv2[:], A.max), "ds2")
+    wait(V, "ds2")
+    done(V.tensor_copy(T.du2[:], T.ds2[:]), "du2")
+    wait(V, "du2", "rr", "cs", "opre2")
+    done(V.tensor_tensor(T.owin[:].indirect(T.du2[:, 0:32]), T.rr[:], T.cwin[:, 0:CC], A.add), "osc")
+    wait(V, "osc")
+    done(V.tensor_copy(T.oi[:], T.owin[:, 0:ZZ]), "oi")
+    wait(V, "oi")
+    done(V.tensor_scalar(T.of[:], T.oi[:], -32.0, None, A.add), "of")
+
+    wait(Y, "of")
+    Y.dma_start(T.yk[:], T.of[1:128:16, :]).then_inc(T.sem.out1, 16)
+    Y.wait_ge(T.sem.out1, 16)
+    wait(S, "of")
+    S.dma_start(T.ys[:], T.of[2:128:16, :]).then_inc(T.sem.out2, 16)
+    S.wait_ge(T.sem.out2, 16)
+    for s in ("osent", "psent", "fs3", "fs2", "fs1"):
+        g.wait_ge(T.sem[s], NEG)

@@ -5,6 +5,7 @@ A = AluOpType
 F = ActivationFunctionType
 NV = 16384
 NE = 2048
+HE = NE // 2
 FILLV = 128.0
 NONE = 16 * 128 + 128
 DW = NONE + 8
@@ -12,22 +13,25 @@ BIG = 8192.0
 HUGE = 65536.0
 CC = 512
 ZZ = 128
-NVEC = 8192
+NVEC = 7168
 NDMA = 4096
+FW = 1024
+ROUND = 8388608.0
 
 
 def _bufs():
     d = {}
     for where, typ, items in (
-            ("sbuf", "int32", "owni:128 nxti:128 ptsi:128 ownr:128 oi:128 pi:1 pm:1"),
+            ("sbuf", "int32", "owni:128 nxti:128 ptsi:128 ownr:128 pi:1 pm:1"),
             ("sbuf", "uint16", "ou:128 nu:128 fu:128 fl1:128 fl2:128 fl3:128 du:128 pu:32 du2:32"),
-            ("sbuf", "bfloat16", "ptsb:128 ptl1:128 ptl2:128 ptl3:128 ptl4:128 ptr1:2048 ptr2:2048 ptr3:2048 ptr4:2048 p1:2048 p2:2048 p3:2048"
+            ("sbuf", "bfloat16", "ptsb:128 p1:2048 p2:2048 p3:2048 w4:%d"
                                  " tab:16384 val:2048 gat:2048 cb:512 ones:512 zb:128 hi:256 lo:256 t1:256 t2:256 bas:256"
-                                 " bd0:128 bd:128 tri:128 upp:128 idb:128 l4:128 eg:8 ww:2048 ka:128 kb2:512 kb3:512 vb:129 vb2:33"),
-            ("sbuf", "float32", "w4:%d d3:%d d2:%d d1:%d ownf:128 ptf:128 tf:128 np:2048 xx:2048 cwin:2560 s1:512 sw:512 rr:512 owin:640 of:128"
-                                " zf:128 pmf:1 c0:1 c1:1 c3:1 co:1 cc:1 wc:1 n1:1 i8:8 bcol:8 idf:128 onef:128 hm:512 ii:128 i512:128 i128:32"
-                                " nv:128 iv:128 xs:128 ds:128 nv2:32 iv2:32 xs2:32 ds2:32" % (DW, DW, DW, DW)),
-            ("psum", "float32", "pspa:1024 pspb:1024 psf0:512 psf1:512 psd:512 psw:512")):
+                                 " bd0:128 bd:128 tri:128 upp:128 eg:8 ww:2048 ka:128 kb2:512 kb3:512 vb:129 vb2:33" % DW),
+            ("sbuf", "float32", "d3:%d d2:%d d1:%d ownf:128 ptf:128 tf:128 np:2048 xx:2048 cwin:2560 s1:512 sw:512 rr:512 owin:640 of:128"
+                                " zf:128 pmf:1 c0:1 c1:1 c3:1 wc:1 n1:1 i8:8 bcol:8 idf:128 onef:128 hm:512 ii:128 i512:128 i128:32"
+                                " iv:128 ds:128 nv2:32 iv2:32 xs2:32 ds2:32" % (DW, DW, DW)),
+            ("dram", "bfloat16", "ptl1:128 ptl2:128 ptl3:128 ptl4:128"),
+            ("psum", "float32", "psf0:512 psf1:512 psd:512 psw:512 psh:512 psr:512")):
         for it in items.split():
             name, w = it.split(":")
             d[name] = (where, [128, int(w)], typ)
@@ -35,11 +39,11 @@ def _bufs():
 
 
 SCRATCH = _bufs()
-EV = """ones tab0 tabv tabs pi pm pmf c0 c1 c3 cc co n1 wc hl t1 t2 bas i8 bcol val onef bd0 bd tri upp idb idf l4 zb zf
-kab ii i512 i128 w4t tails cpre vz opre opre2 np0 ww0 eg ww ownf ptf tr tf psk4 w4 ptsb nu ou scat ga gb fa fb fuv vb nv iv dl xs ds du
-xa xb xx0 xx1 cs0 cs cb pw pu rh hm hmv d3 d2 d1 s1 rr sw vb2 nv2 iv2 dl2 xs2 ds2 du2 osc oi of""".split()
-SEMAPHORES = ["e_" + e for e in EV] + ["ldo", "ldn", "ldp", "dfl", "dnp", "dp4", "dp3", "dp2", "dp1", "rep3", "rep2", "rep1", "oarr", "osent", "parr", "psent",
-                                       "fa1", "fa2", "fa3", "fs1", "fs2", "fs3", "out1", "out2"]
+EV = """ones tab0 tabv tabs pi pm pmf c0 c1 c3 n1 wc hl t1 t2 bas i8 bcol val onef bd0 bd tri upp idf zb zf
+kab ii i512 i128 w4t tails cpre vz opre opre2 ww0 eg ww ownf ptf tr tf ptsb nu ou scat ga gb fa fb fva fvb vb nv iv dl xs ds du
+xc0 xc1 cs0 cs cb pw pu rh hm hmv d3 d2 d1 s1 rr sw vb2 nv2 iv2 dl2 xs2 ds2 du2 osc of""".split()
+SEMAPHORES = ["e_" + e for e in EV] + ["ldo", "ldn", "ldp", "dfl", "dnp", "dx0", "dx1", "rep4", "rep3", "rep2", "rep1", "oarr", "osent", "parr", "psent",
+                                       "fa1", "fa2", "fa3a", "fa3b", "fs1", "fs2", "fs3", "out1", "out2"]
 
 
 def rank_program(g, core, T, topo):
@@ -69,13 +73,13 @@ def rank_program(g, core, T, topo):
     es = set(topo.engines(core, back[1]))
     for k in range(2, n - 1):
         es &= set(topo.engines(core, back[k]))
-    E = sorted(es)[0:8:2]
+    E = sorted(es)[0:8]
     M = sum(1 << e for e in E)
     NEG = len(E)
 
-    def send(buf_out, buf_in, dst, rs, ls):
+    def send(dst_ap, src_ap, dst, rs, ls):
         rid, pid = topo.addr(dst)[:2]
-        g.remote_dma(buf_out[:], buf_in[:], T.sem[rs], T.sem[ls], pid, rid, M)
+        g.remote_dma(dst_ap, src_ap, T.sem[rs], T.sem[ls], pid, rid, M)
 
     Y.dma_start(T.owni[:], T.own[:]).then_inc(T.sem.ldo, 16)
     Y.dma_start(T.ptsi[:], T.pts[:]).then_inc(T.sem.ldp, 16)
@@ -85,12 +89,10 @@ def rank_program(g, core, T, topo):
     done(g.iota(T.i8[:], [[16, 8]], 0, 0, allow_small_or_imprecise_dtypes=True), "i8")
     done(g.iota(T.hi[:], [[1, 16], [0, 16]], 0, 0, allow_small_or_imprecise_dtypes=True), "hl")
     done(g.iota(T.lo[:], [[0, 16], [1, 16]], 0, 0, allow_small_or_imprecise_dtypes=True), "hl")
-    g.wait_ge(T.sem.ldo, 16)
-    send(T.ownr, T.owni, back[1], "oarr", "osent")
     wait(g, "ones")
     done(g.affine_select(T.bd0[:], T.ones[:, 0:128], [[-16, 8], [0, 16]], A.is_ge, 0.0, 0, 1), "bd0")
-    wait(g, "bd0")
-    done(g.affine_select(T.bd[:], T.bd0[:], [[16, 8], [0, 16]], A.is_ge, 0.0, 15, -1), "bd")
+    g.wait_ge(T.sem.ldo, 16)
+    send(T.ownr[:], T.owni[:], back[1], "oarr", "osent")
     wait(g, "ptsb")
     ids, dsts = [], []
     for k in (4, 3, 2, 1):
@@ -98,12 +100,12 @@ def rank_program(g, core, T, topo):
         ids.append(DstId(rid=rid, pnc=pid))
         dsts.append(T["ptl%d" % k][:])
     g.remote_dma_fused([RemoteDMATransfer(dst_ids=ids, dma_engine_mask=M, remote_sem=T.sem.parr, src=T.ptsb[:], dsts=dsts)], local_sem=T.sem.psent)
+    wait(g, "bd0")
+    done(g.affine_select(T.bd[:], T.bd0[:], [[16, 8], [0, 16]], A.is_ge, 0.0, 15, -1), "bd")
     const(T.onef[:], 1, "onef")
     wait(g, "onef")
     done(g.affine_select(T.idf[:], T.onef[:], [[-1, 128]], A.is_equal, 0.0, 0, 1), "idf")
-    const(T.ww[:], 0, "ww0")
-    done(g.affine_select(T.l4[0:8, :], T.ones[0:8, 0:128], [[-1, 8], [0, 16]], A.is_equal, 0.0, 0, 1), "l4")
-    done(g.affine_select(T.idb[:], T.ones[:, 0:128], [[-1, 128]], A.is_equal, 0.0, 0, 1), "idb")
+    const(T.ww[:, 1024:NE], 0, "ww0")
     wait(g, "bd")
     done(g.affine_select(T.tri[:], T.bd[:], [[1, 128]], A.is_gt, 0.0, 0, -1), "tri")
     done(g.affine_select(T.upp[:], T.bd[:], [[-1, 128]], A.is_ge, 0.0, 0, 1), "upp")
@@ -112,10 +114,12 @@ def rank_program(g, core, T, topo):
     const(T.vb[:, 0:1], 0, "vz")
     const(T.vb2[:, 0:1], 0, "vz")
     const(T.w4[:, NE:DW], -BIG, "w4t")
-    wait(g, ("fuv", 2))
-    send(T.fl3, T.fu, back[3], "fa3", "fs3")
-    send(T.fl2, T.fu, back[2], "fa2", "fs2")
-    send(T.fl1, T.fu, back[1], "fa1", "fs1")
+    wait(g, "fva")
+    send(T.fl3[:, 0:64], T.fu[:, 0:64], back[3], "fa3a", "fs3")
+    wait(g, "fvb")
+    send(T.fl3[:, 64:128], T.fu[:, 64:128], back[3], "fa3b", "fs3")
+    send(T.fl2[:], T.fu[:], back[2], "fa2", "fs2")
+    send(T.fl1[:], T.fu[:], back[1], "fa1", "fs1")
     for b in ("d3", "d2", "d1"):
         const(T[b][:, NE:DW], -BIG, "tails")
     const(T.zb[:], 0, "zb")
@@ -126,152 +130,145 @@ def rank_program(g, core, T, topo):
     const(T.owin[:, 0:ZZ], 32, "opre")
 
     wait(Y, "tab0")
-    for a in range(NVEC, NVEC + NDMA, 2048):
-        Y.dma_start(T.tab[:, a:a + 2048], T.tab[:, 0:2048]).then_inc(T.sem.dfl, 16)
-    Y.wait_ge(T.sem.parr, 4 * NEG)
-    for k in (4, 3, 2, 1):
-        Y.dma_start(T["ptr%d" % k][0:8, :], T["ptl%d" % k][:]).then_inc(T.sem["dp%d" % k], 16)
-    wait(Y, "ptf", ("np0", 4))
+    for a in range(NVEC, NVEC + NDMA, FW):
+        Y.dma_start(T.tab[:, a:a + FW], T.tab[:, 0:FW]).then_inc(T.sem.dfl, 16)
+    wait(Y, "ptf")
     Y.dma_start(T.np[2:128:16, :], T.ptf[:]).then_inc(T.sem.dnp, 16)
     wait(Y, "tf")
     for h in range(8):
         Y.dma_start(T.np[16 * h + 1:16 * h + 2, :], T.tf[:, 16 * h:16 * h + 16]).then_inc(T.sem.dnp, 16)
-    for k in (3, 2, 1):
-        Y.wait_ge(T.sem["dp%d" % k], 16)
+    Y.wait_ge(T.sem.parr, 4 * NEG)
+    for k in (4, 3, 2):
         for s in range(16):
-            Y.dma_start(T["p%d" % k][s:128:16, :], T["ptr%d" % k][0:8, :]).then_inc(T.sem["rep%d" % k], 16)
+            Y.dma_start(T["w4" if k == 4 else "p%d" % k][s:128:16, 0:NE], T["ptl%d" % k][:]).then_inc(T.sem["rep%d" % k], 16)
+    Y.wait_ge(T.sem.dnp, 16 * 9)
+    for h in range(2):
+        wait(Y, "xc%d" % h)
+        for row in (1, 2):
+            Y.dma_start(T.xx[row:128:16, HE * h:HE * h + HE], T.np[row:128:16, HE * h:HE * h + HE]).then_inc(T.sem["dx%d" % h], 16)
+    Y.wait_ge(T.sem.fs3, 2 * NEG)
+    for s in range(16):
+        Y.dma_start(T.p1[s:128:16, 0:NE], T.ptl1[:]).then_inc(T.sem.rep1, 16)
 
+    done(V.memset(T.tab[:, 0:FW], FILLV), "tab0")
     done(V.memset(T.ones[:], 1.0), "ones")
-    done(V.memset(T.tab[:, 0:2048], FILLV), "tab0")
     wait(V, "pi")
     done(V.tensor_scalar(T.pm[:], T.pi[:], 15, None, A.bitwise_and), "pm")
     wait(V, "pm")
-    done(V.tensor_copy(T.pmf[:], T.pm[:]), "pmf")
     done(V.tensor_scalar(T.c0[:], T.pm[:], 0.0, None, A.is_equal), "c0")
-    done(V.tensor_scalar(T.c1[:], T.pm[:], 1.0, None, A.is_equal), "c1")
     done(V.tensor_scalar(T.c3[:], T.pm[:], 3.0, None, A.is_equal), "c3")
-    done(V.memset(T.tab[:, 2048:4096], FILLV), "tabv")
-    wait(V, "c0", "c1", "c3")
-    done(V.tensor_tensor(T.cc[:], T.c0[:], T.c3[:], A.add), "cc")
-    done(V.tensor_scalar(T.wc[:], T.c0[:], 16.0, T.c3[:], A.mult, A.add), "wc")
-    wait(V, ("hl", 2), "i8", "cc")
-    done(V.tensor_scalar(T.co[:], T.cc[:], -FILLV, FILLV, A.mult, A.add), "co")
+    done(V.memset(T.tab[:, FW:4096], FILLV), "tabv")
+    wait(V, "c0", "c3", ("hl", 2), "i8")
+    done(V.tensor_scalar(T.bcol[:], T.i8[:], T.c0[:], None, A.mult), "bcol")
     done(V.tensor_scalar(T.t1[:], T.hi[:], T.c0[:], None, A.mult), "t1")
     done(V.tensor_scalar(T.t2[:], T.lo[:], T.c3[:], None, A.mult), "t2")
     V.wait_ge(T.sem.ldp, 16)
     done(V.tensor_copy(T.ptsb[:], T.ptsi[:]), "ptsb")
-    wait(V, "co", "t1", "t2")
+    wait(V, "t1", "t2")
     done(V.tensor_tensor(T.bas[:], T.t1[:], T.t2[:], A.add), "bas")
-    done(V.tensor_scalar(T.bcol[:], T.i8[:], T.c0[:], T.co[:], A.mult, A.add), "bcol")
     wait(V, "bas", "bcol")
     for a in range(8):
         done(V.tensor_scalar(T.val[:, 256 * a:256 * a + 256], T.bas[:], T.bcol[:, a:a + 1], None, A.add), "val")
-    done(V.memset(T.tab[:, 4096:NVEC], FILLV), "tabv")
     V.wait_ge(T.sem.ldo, 16)
-    done(V.tensor_scalar(T.ownf[:], T.owni[:], 16.0 + 16.0 - FILLV, None, A.add), "ownf")
-    wait(V, "bd", "wc")
-    done(V.tensor_scalar(T.eg[:], T.bd[:, 0:128:16], T.wc[:], None, A.mult), "eg")
+    done(V.tensor_scalar(T.ownf[:], T.owni[:], 32.0, None, A.add), "ownf")
+    done(V.memset(T.tab[:, 4096:NVEC], FILLV), "tabv")
     V.wait_ge(T.sem.ldn, 16)
     done(V.tensor_copy(T.nu[:], T.nxti[:]), "nu")
-    done(V.tensor_scalar(T.ptf[:], T.ptsi[:], 16.0 + 16.0 - FILLV, None, A.add), "ptf")
-    done(V.tensor_scalar(T.n1[:], T.c1[:], -1.0, 1.0, A.mult, A.add), "n1")
     V.wait_ge(T.sem.oarr, NEG)
     done(V.tensor_copy(T.ou[:], T.ownr[:]), "ou")
-    wait(V, "ou", ("tabv", 2), ("tabs", 2), ("val", 8), "tab0")
-    V.wait_ge(T.sem.dfl, 16 * (NDMA // 2048))
+    wait(V, "ou", ("tabv", 2), ("tabs", (NV - NVEC - NDMA) // FW), ("val", 8), "tab0")
+    V.wait_ge(T.sem.dfl, 16 * (NDMA // FW))
     done(V.tensor_copy(T.tab[:].indirect(T.ou[:, 0:128]), T.val[:]), "scat")
     wait(V, "scat", "nu")
     done(V.tensor_copy(T.gat[:, 0:512], T.tab[:].indirect(T.nu[:, 0:32])), "ga")
     done(V.tensor_copy(T.gat[:, 1024:1536], T.tab[:].indirect(T.nu[:, 64:96])), "gb")
 
     wait(S, "tab0")
-    for a in range(NVEC + NDMA, NV, 2048):
-        done(S.activation(T.tab[:, a:a + 2048], T.tab[:, 0:2048], F.Silu), "tabs")
+    for a in range(NVEC + NDMA, NV, FW):
+        done(S.activation(T.tab[:, a:a + FW], T.tab[:, 0:FW], F.Copy), "tabs")
+    wait(S, "ptsb", "c0", "c3")
+    done(S.activation(T.ptf[:], T.ptsb[:], F.Identity, bias=32.0), "ptf")
+    done(S.activation(T.wc[:], T.c0[:], F.Identity, bias=T.c3[:], scale=16.0), "wc")
     wait(S, "ones")
-    for a in range(4):
-        done(S.activation(T.np[:, 512 * a:512 * a + 512], T.ones[:], F.Copy, scale=16.0), "np0")
+    for a in (0, 512):
+        done(S.activation(T.ww[:, a:a + 512], T.ones[:], F.Copy, scale=0.0), "ww0")
+    wait(S, "wc", "bd")
+    done(S.activation(T.eg[:], T.bd[:, 0:128:16], F.Copy, scale=T.wc[:]), "eg")
     wait(S, "tr")
     done(S.activation(T.tf[:], T.psd[:, 0:128], F.Copy), "tf")
-    wait(S, "eg", "ww0")
+    wait(S, "eg", ("ww0", 3))
     for s in range(16):
         done(S.activation(T.ww[:, 128 * s + s:128 * s + 128:16], T.eg[:], F.Copy), "ww")
-    done(S.activation(T.cwin[:, 0:CC], T.ones[:], F.Copy, scale=FILLV + 16.0), "cpre")
-    wait(S, ("psk4", 4))
-    done(S.activation(T.w4[:, 0:1024], T.pspa[:], F.Copy), "w4")
-    done(S.activation(T.w4[:, 1024:2048], T.pspb[:], F.Copy), "w4")
+    done(S.activation(T.cwin[:, 0:CC], T.ones[:], F.Silu, scale=FILLV + 16.0), "cpre")
     wait(S, "scat", "nu")
     done(S.activation(T.gat[:, 512:1024], T.tab[:].indirect(T.nu[:, 32:64]), F.Copy), "ga")
     done(S.activation(T.gat[:, 1536:2048], T.tab[:].indirect(T.nu[:, 96:128]), F.Copy), "gb")
-    wait(S, "du", "xx0", "cpre")
-    done(S.activation(T.cwin[:].indirect(T.du[:, 0:64]), T.xx[:, 0:1024], F.Silu), "cs0")
-    wait(S, "cs0", "xx1")
-    done(S.activation(T.cwin[:].indirect(T.du[:, 64:128]), T.xx[:, 1024:2048], F.Silu), "cs")
+    wait(S, ("ga", 2))
+    done(S.activation(T.xx[:, 0:HE], T.gat[:, 0:HE], F.Identity, bias=16.0), "xc0")
+    wait(S, ("gb", 2))
+    done(S.activation(T.xx[:, HE:NE], T.gat[:, HE:NE], F.Identity, bias=16.0), "xc1")
+    wait(S, "du", "cpre")
+    S.wait_ge(T.sem.dx0, 32)
+    done(S.activation(T.cwin[:].indirect(T.du[:, 0:64]), T.xx[:, 0:HE], F.Silu), "cs0")
+    wait(S, "cs0")
+    S.wait_ge(T.sem.dx1, 32)
+    done(S.activation(T.cwin[:].indirect(T.du[:, 64:128]), T.xx[:, HE:NE], F.Silu), "cs")
     wait(S, "cs")
     done(S.activation(T.cb[:], T.cwin[:, 0:CC], F.Copy), "cb")
     wait(S, "hm")
-    done(S.activation(T.hm[:], T.psf1[:], F.Copy), "hmv")
+    done(S.activation(T.hm[:], T.psh[:], F.Copy), "hmv")
     wait(S, "pu", "d1", ("tails", 3), "n1")
     done(S.activation(T.rr[:], T.d1[:].indirect(T.pu[:, 0:32]), F.Identity, scale=T.n1[:]), "rr")
 
     wait(P, "ownf", "idf")
     done(P.transpose(T.psd[:, 0:128], T.ownf[:], T.idf[:]), "tr")
-    P.wait_ge(T.sem.dp4, 16)
-    wait(P, "l4")
-    for b in range(4):
-        ps = (T.pspa, T.pspb)[b // 2]
-        done(P.matmul(ps[:, 512 * (b % 2):512 * (b % 2) + 512], T.l4[0:8, :], T.ptr4[0:8, 512 * b:512 * b + 512], True, True), "psk4")
     for c, (ps, e, e2) in enumerate(((T.psf0, "fa", "ga"), (T.psf1, "fb", "gb"))):
         wait(P, ("ww", 16), (e2, 2))
         for s in range(16):
-            m = P.matmul(ps[:, 0:64], T.ww[:, 128 * s:128 * s + 128], T.gat[:, 1024 * c + s:1024 * c + 1024:16], s == 0, s == 15)
+            m = P.matmul(ps[:, 0:64], T.ww[:, 128 * s:128 * s + 128], T.gat[:, HE * c + s:HE * c + HE:16], s == 0, s == 15)
         done(m, e)
-    wait(P, ("w4", 2), "idb")
-    for b in range(2):
-        done(P.matmul(T.pspa[:, 512 * b:512 * b + 512], T.idb[:], T.gat[:, 512 * b:512 * b + 512], True, True), "xa")
     wait(P, "tri", "upp", ("vb", 2), ("vz", 2), "tf")
     P.matmul(T.psd[:, 0:128], T.tri[:], T.vb[:, 1:129], True, False)
     done(P.matmul(T.psd[:, 0:128], T.upp[:], T.vb[:, 0:128], False, True), "dl")
-    for b in range(2):
-        done(P.matmul(T.pspb[:, 512 * b:512 * b + 512], T.idb[:], T.gat[:, 1024 + 512 * b:1536 + 512 * b], True, True), "xb")
-    wait(P, ("kab", 3), ("fuv", 2), ("vb", 2), ("nv", 2))
-    done(P.matmul(T.psf1[:], T.ka[0:16, :], T.kb3[0:16, :], True, True), "hm")
-    done(P.matmul(T.psf0[:], T.ka[0:16, :], T.kb2[0:16, :], True, True), "rh")
-    wait(P, "cb")
+    wait(P, ("kab", 3))
+    done(P.matmul(T.psh[:], T.ka[0:16, :], T.kb3[0:16, :], True, True), "hm")
+    done(P.matmul(T.psr[:], T.ka[0:16, :], T.kb2[0:16, :], True, True), "rh")
+    wait(P, "cb", "iv")
     for s in range(16):
         m = P.matmul(T.psw[:, 0:32], T.ww[:, 128 * s:128 * s + 128], T.cb[:, s:CC:16], s == 0, s == 15)
     done(m, "pw")
-    wait(P, "vb2", "xs")
+    wait(P, "vb2", "ds")
     P.matmul(T.psd[:, 0:32], T.tri[:], T.vb2[:, 1:33], True, False)
     done(P.matmul(T.psd[:, 0:32], T.upp[:], T.vb2[:, 0:32], False, True), "dl2")
 
-    wait(V, "ii", "pmf")
+    done(V.tensor_copy(T.pmf[:], T.pm[:]), "pmf")
+    done(V.tensor_scalar(T.c1[:], T.pm[:], 1.0, None, A.is_equal), "c1")
+    wait(V, "ii", "pmf", "c1")
     done(V.tensor_scalar(T.i512[:], T.ii[:], T.pmf[:], None, A.add), "i512")
     done(V.tensor_scalar(T.i128[:], T.ii[:, 0:32], T.pmf[:], float(ZZ - CC), A.add, A.add), "i128")
-    for c, (ps, e) in enumerate(((T.psf0, "fa"), (T.psf1, "fb"))):
+    done(V.tensor_scalar(T.n1[:], T.c1[:], -1.0, 1.0, A.mult, A.add), "n1")
+    for c, (ps, e, e2) in enumerate(((T.psf0, "fa", "fva"), (T.psf1, "fb", "fvb"))):
         wait(V, e)
-        done(V.tensor_copy(T.fu[:, 64 * c:64 * c + 64], ps[:, 0:64]), "fuv")
+        done(V.tensor_copy(T.fu[:, 64 * c:64 * c + 64], ps[:, 0:64]), e2)
         done(V.tensor_scalar(T.vb[:, 1 + 64 * c:65 + 64 * c], ps[:, 0:64], float(NE), None, A.is_lt), "vb")
-        done(V.tensor_scalar(T.nv[:, 64 * c:64 * c + 64], ps[:, 0:64], float(NE), None, A.is_ge), "nv")
+        done(V.tensor_scalar(T.psw[:, 64 * c:64 * c + 64], ps[:, 0:64], float(NE), None, A.is_ge), "nv")
     wait(V, ("nv", 2), "i512")
-    done(V.tensor_tensor(T.iv[:], T.nv[:], T.i512[:], A.mult), "iv")
-    V.wait_ge(T.sem.dnp, 16 * 9)
-    wait(V, ("xa", 2))
-    done(V.tensor_tensor(T.xx[:, 0:1024], T.pspa[:], T.np[:, 0:1024], A.add), "xx0")
+    done(V.tensor_tensor(T.iv[:], T.psw[:, 0:128], T.i512[:], A.mult), "iv")
     wait(V, "dl", "zf")
-    done(V.tensor_tensor_scan(T.xs[:], T.psd[:, 0:128], T.zf[:], 0.0, A.add, A.add), "xs")
+    done(V.tensor_tensor_scan(T.psd[:, 128:256], T.psd[:, 0:128], T.zf[:], 0.0, A.add, A.add), "xs")
     wait(V, "xs", "iv")
-    done(V.tensor_tensor(T.ds[:], T.xs[:], T.iv[:], A.max), "ds")
+    done(V.tensor_tensor(T.ds[:], T.psd[:, 128:256], T.iv[:], A.max), "ds")
     wait(V, "ds")
     done(V.tensor_copy(T.du[:], T.ds[:]), "du")
-    wait(V, ("xb", 2))
-    done(V.tensor_tensor(T.xx[:, 1024:2048], T.pspb[:], T.np[:, 1024:2048], A.add), "xx1")
-    V.wait_ge(T.sem.fa3, NEG)
+    V.wait_ge(T.sem.rep4, 256)
     V.wait_ge(T.sem.rep3, 256)
-    wait(V, ("w4", 2), "w4t")
-    done(V.tensor_tensor(T.d3[:, 0:NE], T.w4[:].indirect(T.fl3[:, 0:128]), T.p3[:], A.add), "d3")
+    wait(V, "w4t")
+    for h, rs in enumerate(("fa3a", "fa3b")):
+        V.wait_ge(T.sem[rs], NEG)
+        done(V.tensor_tensor(T.d3[:, HE * h:HE * h + HE], T.w4[:].indirect(T.fl3[:, 64 * h:64 * h + 64]), T.p3[:, HE * h:HE * h + HE], A.add), "d3")
     V.wait_ge(T.sem.fa2, NEG)
     V.wait_ge(T.sem.rep2, 256)
-    wait(V, ("tails", 3), "d3")
+    wait(V, ("tails", 3), ("d3", 2))
     done(V.tensor_tensor(T.d2[:, 0:NE], T.d3[:].indirect(T.fl2[:, 0:128]), T.p2[:], A.add), "d2")
     V.wait_ge(T.sem.fa1, NEG)
     V.wait_ge(T.sem.rep1, 256)
@@ -282,7 +279,7 @@ def rank_program(g, core, T, topo):
     wait(V, "pu", "d1", "hmv")
     done(V.tensor_tensor(T.s1[:], T.d1[:].indirect(T.pu[:, 0:32]), T.hm[:], A.add), "s1")
     wait(V, "s1", "rh")
-    done(V.tensor_tensor_scan(T.sw[:], T.psf0[:], T.s1[:], 0.0, A.max, A.min), "sw")
+    done(V.tensor_tensor_scan(T.sw[:], T.psr[:], T.s1[:], 0.0, A.max, A.min), "sw")
     wait(V, "sw")
     done(V.tensor_scalar(T.vb2[:, 1:33], T.sw[:, 15:CC:16], 0.0, None, A.is_ge), "vb2")
     done(V.tensor_scalar(T.nv2[:], T.sw[:, 15:CC:16], 0.0, None, A.is_lt), "nv2")
@@ -299,9 +296,7 @@ def rank_program(g, core, T, topo):
     wait(V, "du2", "rr", "cs", "opre2")
     done(V.tensor_tensor(T.owin[:].indirect(T.du2[:, 0:32]), T.rr[:], T.cwin[:, 0:CC], A.add), "osc")
     wait(V, "osc")
-    done(V.tensor_copy(T.oi[:], T.owin[:, 0:ZZ]), "oi")
-    wait(V, "oi")
-    done(V.tensor_scalar(T.of[:], T.oi[:], -32.0, None, A.add), "of")
+    done(V.tensor_scalar(T.of[:], T.owin[:, 0:ZZ], ROUND, ROUND + 32.0, A.add, A.subtract), "of")
 
     wait(Y, "of")
     Y.dma_start(T.yk[:], T.of[1:128:16, :]).then_inc(T.sem.out1, 16)
@@ -310,4 +305,4 @@ def rank_program(g, core, T, topo):
     S.dma_start(T.ys[:], T.of[2:128:16, :]).then_inc(T.sem.out2, 16)
     S.wait_ge(T.sem.out2, 16)
     for s in ("osent", "psent", "fs3", "fs2", "fs1"):
-        g.wait_ge(T.sem[s], NEG)
+        g.wait_ge(T.sem[s], 2 * NEG if s == "fs3" else NEG)

@@ -6,15 +6,20 @@ F = ActivationFunctionType
 NV = 16384
 NE = 2048
 HE = NE // 2
-FILLV = 128.0
-NONE = 16 * 128 + 128
-DW = NONE + 8
+QE = NE // 4
+CH = 256
 BIG = 8192.0
-HUGE = 65536.0
+PF = 8.0
+NONE = 8 * CH + 8
+DW = NONE + 8
 CC = 512
+HC = CC // 2
 ZZ = 128
-NVEC = 7168
+SH = 16.0
+NA = 576
+NVEC = 6656
 NDMA = 4096
+NGP = 1024
 FW = 1024
 ROUND = 8388608.0
 
@@ -22,16 +27,15 @@ ROUND = 8388608.0
 def _bufs():
     d = {}
     for where, typ, items in (
-            ("sbuf", "int32", "owni:128 nxti:128 ptsi:128 ownr:128 pi:1 pm:1"),
-            ("sbuf", "uint16", "ou:128 nu:128 fu:128 fl1:128 fl2:128 fl3:128 du:128 pu:32 du2:32"),
-            ("sbuf", "bfloat16", "ptsb:128 p1:2048 p2:2048 p3:2048 w4:%d"
-                                 " tab:16384 val:2048 gat:2048 cb:512 ones:512 zb:128 hi:256 lo:256 t1:256 t2:256 bas:256"
-                                 " bd0:128 bd:128 tri:128 upp:128 eg:8 ww:2048 ka:128 kb2:512 kb3:512 vb:129 vb2:33" % DW),
-            ("sbuf", "float32", "d3:%d d2:%d d1:%d ownf:128 ptf:128 tf:128 np:2048 xx:2048 cwin:2560 s1:512 sw:512 rr:512 owin:640 of:128"
-                                " zf:128 pmf:1 c0:1 c1:1 c3:1 wc:1 n1:1 i8:8 bcol:8 idf:128 onef:128 hm:512 ii:128 i512:128 i128:32"
-                                " iv:128 ds:128 nv2:32 iv2:32 xs2:32 ds2:32" % (DW, DW, DW)),
-            ("dram", "bfloat16", "ptl1:128 ptl2:128 ptl3:128 ptl4:128"),
-            ("psum", "float32", "psf0:512 psf1:512 psd:512 psw:512 psh:512 psr:512")):
+            ("sbuf", "int32", "owni:128 nxti:128 ptsi:128 pi:1 pm:1"),
+            ("sbuf", "uint16", "ou:128 nu:128 nr:128 fu:128 fl1:128 fl2:128 du:128 pu:32 ic:32 du2:32"),
+            ("sbuf", "bfloat16", "ptsb:128 xl1:128 p1:2048 w3:%d tab:16384 val:2048 gat:2048 lo:256 ipat:%d ca:%d cb:512 kk:512 ones:128"
+                                 " bd0:128 bd:128 tri:128 upp:128 za:144 zi:144 zk:144 vb:129 vb2:33" % (DW, NA, CC + NA)),
+            ("sbuf", "float32", "b2:%d b1:%d xx:%d ownf:128 ptf:128 tf:128 ilo:512 cwin:2560 rr:512 cw:512 owin:640"
+                                " zf:128 pmf:1 c0:1 c1:1 c2:1 c3:1 c1n:1 c2n:1 wc:1 wi:1 n1:1 i8:8 bcol:8 bco1:8 bcn:8 idf:128 onef:128"
+                                " ii:128 i512:128 i128:32 iv:128 ds:128 nv2:32 iv2:32 xs2:32 ds2:32 puf:32 icf:32 pur:32 icr:32" % (DW, DW, DW)),
+            ("dram", "bfloat16", "xo:128 xl2:128 xl3:128 xl4:128"),
+            ("psum", "float32", "psf0:512 psf1:512 psd:512 psw:512 psi:512 psk:512 pst:512")):
         for it in items.split():
             name, w = it.split(":")
             d[name] = (where, [128, int(w)], typ)
@@ -39,11 +43,11 @@ def _bufs():
 
 
 SCRATCH = _bufs()
-EV = """ones tab0 tabv tabs pi pm pmf c0 c1 c3 n1 wc hl t1 t2 bas i8 bcol val onef bd0 bd tri upp idf zb zf
-kab ii i512 i128 w4t tails cpre vz opre opre2 ww0 eg ww ownf ptf tr tf ptsb nu ou scat ga gb fa fb fva fvb vb nv iv dl xs ds du
-xc0 xc1 cs0 cs cb pw pu rh hm hmv d3 d2 d1 s1 rr sw vb2 nv2 iv2 dl2 xs2 ds2 du2 osc of""".split()
-SEMAPHORES = ["e_" + e for e in EV] + ["ldo", "ldn", "ldp", "dfl", "dnp", "dx0", "dx1", "rep4", "rep3", "rep2", "rep1", "oarr", "osent", "parr", "psent",
-                                       "fa1", "fa2", "fa3a", "fa3b", "fs1", "fs2", "fs3", "out1", "out2"]
+EV = """ones tabg tab0 tabv tabs pi pm pmf c0 c1 c2 c3 cn n1 wc lo ilo i8 bcol bco1 bcn val onef bd0 bd tri upp idf zf z0 za zi zk ipat cap xxi
+ii i512 i128 w3t tails cpre vz opre ownf ptf tr tf ptsb nu ou scat ga gb fa fb fu vb nv iv dl xs ds du
+xc0 xc1 csa cs0 cs cb pw pq puf icf pu ic kk pk b2 b1 rr cw vb2 nv2 iv2 dl2 xs2 ds2 du2 osc""".split()
+SEMAPHORES = ["e_" + e for e in EV] + ["ldo", "ldn", "ldp", "dfl", "dvl", "din", "dxo", "dnp", "dx0", "dx1", "dr1", "dr2", "dr3", "dpt", "narr", "nsent",
+                                       "xa1", "xa2", "xa3", "xa4", "xsent", "fa1", "fa2", "fs1", "fs2", "qa1", "qa2", "qs1", "qs2", "out1", "out2"]
 
 
 def rank_program(g, core, T, topo):
@@ -53,6 +57,7 @@ def rank_program(g, core, T, topo):
     n = len(T.cores)
     V, S, P, Y = g.vector, g.scalar, g.tensor, g.sync
     back = [T.cores[(rank - k) % n] for k in range(n)]
+    after = T.cores[(rank + 1) % n]
 
     def sem(e):
         return T.sem["e_" + e]
@@ -70,8 +75,8 @@ def rank_program(g, core, T, topo):
     def const(buf, v, e):
         done(g.iota(buf, [[0, buf.shape[1]]], int(v), 0, allow_small_or_imprecise_dtypes=True), e)
 
-    es = set(topo.engines(core, back[1]))
-    for k in range(2, n - 1):
+    es = set(topo.engines(core, after))
+    for k in range(1, n - 1):
         es &= set(topo.engines(core, back[k]))
     E = sorted(es)[0:8]
     M = sum(1 << e for e in E)
@@ -81,31 +86,30 @@ def rank_program(g, core, T, topo):
         rid, pid = topo.addr(dst)[:2]
         g.remote_dma(dst_ap, src_ap, T.sem[rs], T.sem[ls], pid, rid, M)
 
+    def send_x(k1, k2):
+        tr = []
+        for k, half in ((k1, E[:NEG // 2]), (k2, E[NEG // 2:])):
+            rid, pid = topo.addr(back[k])[:2]
+            tr.append(RemoteDMATransfer(dst_ids=[DstId(rid=rid, pnc=pid)], dma_engine_mask=sum(1 << e for e in half), remote_sem=T.sem["xa%d" % k],
+                                        srcs=[T.xo[:]], dsts=[T["xl%d" % k][:]]))
+        g.remote_dma_fused(tr, local_sem=T.sem.xsent)
+
     Y.dma_start(T.owni[:], T.own[:]).then_inc(T.sem.ldo, 16)
-    Y.dma_start(T.ptsi[:], T.pts[:]).then_inc(T.sem.ldp, 16)
     S.dma_start(T.nxti[:], T.nxt[:]).then_inc(T.sem.ldn, 16)
+    Y.dma_start(T.ptsi[:], T.pts[:]).then_inc(T.sem.ldp, 16)
 
     done(g.iota(T.pi[:], [[0, 1]], 0, 1), "pi")
-    done(g.iota(T.i8[:], [[16, 8]], 0, 0, allow_small_or_imprecise_dtypes=True), "i8")
-    done(g.iota(T.hi[:], [[1, 16], [0, 16]], 0, 0, allow_small_or_imprecise_dtypes=True), "hl")
-    done(g.iota(T.lo[:], [[0, 16], [1, 16]], 0, 0, allow_small_or_imprecise_dtypes=True), "hl")
+    done(g.iota(T.i8[:], [[1, 8]], 0, 0, allow_small_or_imprecise_dtypes=True), "i8")
+    done(g.iota(T.lo[:], [[1, CH]], 0, 0, allow_small_or_imprecise_dtypes=True), "lo")
+    const(T.tab[:, NVEC + NDMA:NVEC + NDMA + NGP], -BIG, "tabg")
+    wait(g, "nu")
+    send(T.nr[:], T.nu[:], after, "narr", "nsent")
+    const(T.ones[:], 1, "ones")
     wait(g, "ones")
-    done(g.affine_select(T.bd0[:], T.ones[:, 0:128], [[-16, 8], [0, 16]], A.is_ge, 0.0, 0, 1), "bd0")
-    g.wait_ge(T.sem.ldo, 16)
-    send(T.ownr[:], T.owni[:], back[1], "oarr", "osent")
-    wait(g, "ptsb")
-    ids, dsts = [], []
-    for k in (4, 3, 2, 1):
-        rid, pid = topo.addr(back[k])[:2]
-        ids.append(DstId(rid=rid, pnc=pid))
-        dsts.append(T["ptl%d" % k][:])
-    g.remote_dma_fused([RemoteDMATransfer(dst_ids=ids, dma_engine_mask=M, remote_sem=T.sem.parr, src=T.ptsb[:], dsts=dsts)], local_sem=T.sem.psent)
+    done(g.affine_select(T.bd0[:], T.ones[:], [[-16, 8], [0, 16]], A.is_ge, 0.0, 0, 1), "bd0")
     wait(g, "bd0")
     done(g.affine_select(T.bd[:], T.bd0[:], [[16, 8], [0, 16]], A.is_ge, 0.0, 15, -1), "bd")
-    const(T.onef[:], 1, "onef")
-    wait(g, "onef")
-    done(g.affine_select(T.idf[:], T.onef[:], [[-1, 128]], A.is_equal, 0.0, 0, 1), "idf")
-    const(T.ww[:, 1024:NE], 0, "ww0")
+    const(T.za[:], 0, "z0")
     wait(g, "bd")
     done(g.affine_select(T.tri[:], T.bd[:], [[1, 128]], A.is_gt, 0.0, 0, -1), "tri")
     done(g.affine_select(T.upp[:], T.bd[:], [[-1, 128]], A.is_ge, 0.0, 0, 1), "upp")
@@ -113,196 +117,241 @@ def rank_program(g, core, T, topo):
     const(T.zf[:], 0, "zf")
     const(T.vb[:, 0:1], 0, "vz")
     const(T.vb2[:, 0:1], 0, "vz")
-    const(T.w4[:, NE:DW], -BIG, "w4t")
-    wait(g, "fva")
-    send(T.fl3[:, 0:64], T.fu[:, 0:64], back[3], "fa3a", "fs3")
-    wait(g, "fvb")
-    send(T.fl3[:, 64:128], T.fu[:, 64:128], back[3], "fa3b", "fs3")
-    send(T.fl2[:], T.fu[:], back[2], "fa2", "fs2")
-    send(T.fl1[:], T.fu[:], back[1], "fa1", "fs1")
-    for b in ("d3", "d2", "d1"):
+    done(g.iota(T.ilo[0:8, :], [[0, QE // CH], [1, CH]], int(SH), 0, allow_small_or_imprecise_dtypes=True), "ilo")
+    wait(g, "za")
+    const(T.zi[:], 0, "z0")
+    const(T.zk[:], 0, "z0")
+    const(T.w3[:, NE:DW], -BIG, "w3t")
+    g.wait_ge(T.sem.dxo, 16)
+    send_x(4, 3)
+    wait(g, ("fu", 2))
+    send(T.fl2[:], T.fu[:], back[3], "fa2", "fs2")
+    send(T.fl1[:], T.fu[:], back[2], "fa1", "fs1")
+    send_x(2, 1)
+    for b in ("b2", "b1"):
         const(T[b][:, NE:DW], -BIG, "tails")
-    const(T.zb[:], 0, "zb")
-    wait(g, "zb")
-    done(g.affine_select(T.ka[0:16, :], T.zb[0:16, :], [[0, 8], [1, 16]], A.not_equal, HUGE, 0, -1), "kab")
-    done(g.affine_select(T.kb3[0:16, :], T.ones[0:16, :], [[0, 32], [1, 16]], A.not_equal, 0.0, 0, -1), "kab")
-    done(g.affine_select(T.kb2[0:16, :], T.ones[0:16, :], [[0, 32], [1, 16]], A.is_equal, -1.0, 0, -1), "kab")
-    const(T.owin[:, 0:ZZ], 32, "opre")
+    const(T.onef[:], 1, "onef")
+    wait(g, "onef")
+    done(g.affine_select(T.idf[:], T.onef[:], [[-1, 128]], A.is_equal, 0.0, 0, 1), "idf")
+    const(T.xx[:, 0:NA], 0, "xxi")
+    const(T.xx[:, NE:DW], 0, "xxi")
+    wait(g, "ptf")
+    g.wait_ge(T.sem.xa1, NEG // 2)
+    g.dma_start(T.ptf[:], T.xl1[:], accum_op=A.add).then_inc(T.sem.dpt, 16)
+    wait(g, "puf")
+    send(T.pur[:], T.puf[:], back[1], "qa1", "qs1")
+    wait(g, "icf")
+    send(T.icr[:], T.icf[:], back[1], "qa2", "qs2")
 
     wait(Y, "tab0")
     for a in range(NVEC, NVEC + NDMA, FW):
         Y.dma_start(T.tab[:, a:a + FW], T.tab[:, 0:FW]).then_inc(T.sem.dfl, 16)
-    wait(Y, "ptf")
-    Y.dma_start(T.np[2:128:16, :], T.ptf[:]).then_inc(T.sem.dnp, 16)
-    wait(Y, "tf")
+    wait(Y, "ptsb", ("val", 8))
+    Y.dma_start(T.val[4:128:16, :], T.ptsb[:]).then_inc(T.sem.dvl, 16)
+    Y.wait_ge(T.sem.dvl, 16)
+    Y.dma_start(T.w3[:, 0:NE], T.val[:]).then_inc(T.sem.din, 16)
+    Y.dma_start(T.p1[:], T.val[:]).then_inc(T.sem.din, 16)
+    wait(Y, ("ga", 2), ("gb", 2))
+    Y.dma_start(T.xo[:], T.gat[4:128:16, :]).then_inc(T.sem.dxo, 16)
+    wait(Y, "ilo")
+    cuts0 = [NA] + list(range(CH * (NA // CH) + CH, HE + 1, CH))
+    pieces = ([(NA, QE)] if NA < QE else []) + [(max(NA, QE), HE)]
+    for h, cuts, nx in ((0, pieces, len(cuts0) - 1), (1, [(HE, HE + QE), (HE + QE, NE)], HE // CH)):
+        wait(Y, ("xc%d" % h, nx))
+        for a, b in cuts:
+            Y.dma_start(T.xx[2:128:16, a:b], T.ilo[0:8, a % CH:a % CH + b - a]).then_inc(T.sem["dx%d" % h], 16)
+    Y.wait_ge(T.sem.din, 32)
+    wait(Y, "scat", "cpre", "cap", "opre")
+    Y.wait_ge(T.sem.xa4, NEG // 2)
+    Y.dma_start(T.w3[2:128:16, 0:NE], T.xl4[:]).then_inc(T.sem.dr3, 16)
+    Y.wait_ge(T.sem.xa3, NEG // 2)
+    Y.dma_start(T.val[2:128:16, :], T.xl3[:]).then_inc(T.sem.dr2, 16)
+    Y.wait_ge(T.sem.xa2, NEG // 2)
+    Y.dma_start(T.p1[2:128:16, :], T.xl2[:]).then_inc(T.sem.dr1, 16)
+    wait(Y, "cs", ("xxi", 2), "tf")
     for h in range(8):
-        Y.dma_start(T.np[16 * h + 1:16 * h + 2, :], T.tf[:, 16 * h:16 * h + 16]).then_inc(T.sem.dnp, 16)
-    Y.wait_ge(T.sem.parr, 4 * NEG)
-    for k in (4, 3, 2):
-        for s in range(16):
-            Y.dma_start(T["w4" if k == 4 else "p%d" % k][s:128:16, 0:NE], T["ptl%d" % k][:]).then_inc(T.sem["rep%d" % k], 16)
-    Y.wait_ge(T.sem.dnp, 16 * 9)
-    for h in range(2):
-        wait(Y, "xc%d" % h)
-        for row in (1, 2):
-            Y.dma_start(T.xx[row:128:16, HE * h:HE * h + HE], T.np[row:128:16, HE * h:HE * h + HE]).then_inc(T.sem["dx%d" % h], 16)
-    Y.wait_ge(T.sem.fs3, 2 * NEG)
-    for s in range(16):
-        Y.dma_start(T.p1[s:128:16, 0:NE], T.ptl1[:]).then_inc(T.sem.rep1, 16)
+        Y.dma_start(T.xx[16 * h + 1:16 * h + 2, 0:NE], T.tf[:, 16 * h:16 * h + 16]).then_inc(T.sem.dnp, 16)
+    Y.wait_ge(T.sem.dpt, 16)
+    Y.dma_start(T.xx[2:128:16, 0:NE], T.ptf[:]).then_inc(T.sem.dnp, 16)
 
-    done(V.memset(T.tab[:, 0:FW], FILLV), "tab0")
-    done(V.memset(T.ones[:], 1.0), "ones")
+    done(V.memset(T.tab[:, 0:FW], -BIG), "tab0")
     wait(V, "pi")
     done(V.tensor_scalar(T.pm[:], T.pi[:], 15, None, A.bitwise_and), "pm")
     wait(V, "pm")
-    done(V.tensor_scalar(T.c0[:], T.pm[:], 0.0, None, A.is_equal), "c0")
-    done(V.tensor_scalar(T.c3[:], T.pm[:], 3.0, None, A.is_equal), "c3")
-    done(V.memset(T.tab[:, FW:4096], FILLV), "tabv")
-    wait(V, "c0", "c3", ("hl", 2), "i8")
+    for k in (0, 3):
+        done(V.tensor_scalar(T["c%d" % k][:], T.pm[:], float(k), -1.0, A.is_equal, A.mult), "c%d" % k)
+    for k in (1, 2):
+        done(V.tensor_scalar(T["c%d" % k][:], T.pm[:], float(k), None, A.is_equal), "c%d" % k)
+    wait(V, "i8", "c0")
     done(V.tensor_scalar(T.bcol[:], T.i8[:], T.c0[:], None, A.mult), "bcol")
-    done(V.tensor_scalar(T.t1[:], T.hi[:], T.c0[:], None, A.mult), "t1")
-    done(V.tensor_scalar(T.t2[:], T.lo[:], T.c3[:], None, A.mult), "t2")
+    wait(V, "lo", "c3", "bcol")
+    for a in range(8):
+        if a == 4:
+            V.wait_ge(T.sem.ldn, 16)
+            done(V.tensor_copy(T.nu[:], T.nxti[:]), "nu")
+        done(V.tensor_scalar(T.val[:, CH * a:CH * a + CH], T.lo[:], T.c3[:], T.bcol[:, a:a + 1], A.mult, A.add), "val")
     V.wait_ge(T.sem.ldp, 16)
     done(V.tensor_copy(T.ptsb[:], T.ptsi[:]), "ptsb")
-    wait(V, "t1", "t2")
-    done(V.tensor_tensor(T.bas[:], T.t1[:], T.t2[:], A.add), "bas")
-    wait(V, "bas", "bcol")
-    for a in range(8):
-        done(V.tensor_scalar(T.val[:, 256 * a:256 * a + 256], T.bas[:], T.bcol[:, a:a + 1], None, A.add), "val")
     V.wait_ge(T.sem.ldo, 16)
-    done(V.tensor_scalar(T.ownf[:], T.owni[:], 32.0, None, A.add), "ownf")
-    done(V.memset(T.tab[:, 4096:NVEC], FILLV), "tabv")
-    V.wait_ge(T.sem.ldn, 16)
-    done(V.tensor_copy(T.nu[:], T.nxti[:]), "nu")
-    V.wait_ge(T.sem.oarr, NEG)
-    done(V.tensor_copy(T.ou[:], T.ownr[:]), "ou")
-    wait(V, "ou", ("tabv", 2), ("tabs", (NV - NVEC - NDMA) // FW), ("val", 8), "tab0")
+    done(V.tensor_copy(T.ou[:], T.owni[:]), "ou")
+    done(V.memset(T.tab[:, FW:NVEC], -BIG), "tabv")
+    scuts = list(range(NVEC + NDMA + NGP, NV, FW)) + [NV]
+    wait(V, "ou", "tabv", "tabg", ("tabs", len(scuts) - 1), ("val", 8), "tab0")
+    V.wait_ge(T.sem.dvl, 16)
     V.wait_ge(T.sem.dfl, 16 * (NDMA // FW))
     done(V.tensor_copy(T.tab[:].indirect(T.ou[:, 0:128]), T.val[:]), "scat")
-    wait(V, "scat", "nu")
-    done(V.tensor_copy(T.gat[:, 0:512], T.tab[:].indirect(T.nu[:, 0:32])), "ga")
-    done(V.tensor_copy(T.gat[:, 1024:1536], T.tab[:].indirect(T.nu[:, 64:96])), "gb")
+    wait(V, "scat")
+    V.wait_ge(T.sem.narr, NEG)
+    done(V.tensor_copy(T.gat[:, 0:512], T.tab[:].indirect(T.nr[:, 0:32])), "ga")
+    done(V.tensor_copy(T.gat[:, 1024:1536], T.tab[:].indirect(T.nr[:, 64:96])), "gb")
 
     wait(S, "tab0")
-    for a in range(NVEC + NDMA, NV, FW):
-        done(S.activation(T.tab[:, a:a + FW], T.tab[:, 0:FW], F.Copy), "tabs")
-    wait(S, "ptsb", "c0", "c3")
-    done(S.activation(T.ptf[:], T.ptsb[:], F.Identity, bias=32.0), "ptf")
-    done(S.activation(T.wc[:], T.c0[:], F.Identity, bias=T.c3[:], scale=16.0), "wc")
-    wait(S, "ones")
-    for a in (0, 512):
-        done(S.activation(T.ww[:, a:a + 512], T.ones[:], F.Copy, scale=0.0), "ww0")
-    wait(S, "wc", "bd")
-    done(S.activation(T.eg[:], T.bd[:, 0:128:16], F.Copy, scale=T.wc[:]), "eg")
-    wait(S, "tr")
-    done(S.activation(T.tf[:], T.psd[:, 0:128], F.Copy), "tf")
-    wait(S, "eg", ("ww0", 3))
-    for s in range(16):
-        done(S.activation(T.ww[:, 128 * s + s:128 * s + 128:16], T.eg[:], F.Copy), "ww")
-    done(S.activation(T.cwin[:, 0:CC], T.ones[:], F.Silu, scale=FILLV + 16.0), "cpre")
-    wait(S, "scat", "nu")
-    done(S.activation(T.gat[:, 512:1024], T.tab[:].indirect(T.nu[:, 32:64]), F.Copy), "ga")
-    done(S.activation(T.gat[:, 1536:2048], T.tab[:].indirect(T.nu[:, 96:128]), F.Copy), "gb")
-    wait(S, ("ga", 2))
-    done(S.activation(T.xx[:, 0:HE], T.gat[:, 0:HE], F.Identity, bias=16.0), "xc0")
-    wait(S, ("gb", 2))
-    done(S.activation(T.xx[:, HE:NE], T.gat[:, HE:NE], F.Identity, bias=16.0), "xc1")
+    for a, b in zip(scuts, scuts[1:]):
+        done(S.activation(T.tab[:, a:b], T.tab[:, 0:b - a], F.Copy), "tabs")
+    wait(S, "c0", "c1", "c2", "c3", "i8")
+    done(S.activation(T.wc[:], T.c0[:], F.Identity, bias=T.c3[:], scale=float(CH)), "wc")
+    done(S.activation(T.c1n[:], T.c1[:], F.Copy, scale=-1.0), "cn")
+    done(S.activation(T.c2n[:], T.c2[:], F.Copy, scale=-1.0), "cn")
+    done(S.activation(T.bco1[:], T.i8[:], F.Identity, bias=SH, scale=T.c1[:]), "bco1")
+    wait(S, ("cn", 2))
+    done(S.activation(T.wi[:], T.c1n[:], F.Identity, bias=T.c2n[:], scale=float(CH)), "wc")
+    done(S.activation(T.bcn[:], T.i8[:], F.Copy, scale=T.c1n[:]), "bcn")
+    wait(S, "lo", "bcn")
+    ni = 0
+    for a in range(0, NA, CH):
+        b = min(a + CH, NA)
+        done(S.activation(T.ipat[:, a:b], T.lo[:, 0:b - a], F.Identity, bias=T.bcn[:, a // CH:a // CH + 1], scale=T.c2n[:]), "ipat")
+        ni += 1
+    wait(S, ("val", 8))
+    S.wait_ge(T.sem.dvl, 16)
+    done(S.activation(T.cwin[:, 0:CC], T.val[:, 0:CC], F.Silu, bias=SH + PF, scale=0.0), "cpre")
+    done(S.activation(T.ca[:, 0:CC], T.val[:, 0:CC], F.Identity, bias=-PF, scale=0.0), "cap")
+    wait(S, ("wc", 2), "bd", "z0")
+    done(S.activation(T.za[:, 15:143:16], T.bd[:, 0:128:16], F.Copy, scale=T.wc[:]), "za")
+    done(S.activation(T.owin[:, 0:ZZ], T.val[:, 0:ZZ], F.Identity, bias=T.c1n[:], scale=0.0), "opre")
+    wait(S, "ptsb")
+    done(S.activation(T.ptf[:], T.ptsb[:], F.Copy), "ptf")
+    wait(S, "scat")
+    S.wait_ge(T.sem.narr, NEG)
+    done(S.activation(T.gat[:, 512:1024], T.tab[:].indirect(T.nr[:, 32:64]), F.Copy), "ga")
+    done(S.activation(T.gat[:, 1536:2048], T.tab[:].indirect(T.nr[:, 96:128]), F.Copy), "gb")
+    wait(S, ("ga", 2), "bco1")
+    for h, cuts in ((0, cuts0), (1, list(range(HE, NE + 1, CH)))):
+        if h:
+            wait(S, ("gb", 2))
+        for a, b in zip(cuts, cuts[1:]):
+            done(S.activation(T.xx[:, a:b], T.gat[:, a:b], F.Identity, bias=T.bco1[:, a // CH:a // CH + 1], scale=-1.0), "xc%d" % h)
+    wait(S, ("z0", 3))
+    done(S.activation(T.zi[:, 15:143:16], T.bd[:, 0:128:16], F.Copy, scale=T.wi[:]), "zi")
+    done(S.activation(T.zk[:, 15:143:16], T.bd[:, 0:128:16], F.Copy, scale=T.c2[:]), "zk")
     wait(S, "du", "cpre")
-    S.wait_ge(T.sem.dx0, 32)
-    done(S.activation(T.cwin[:].indirect(T.du[:, 0:64]), T.xx[:, 0:HE], F.Silu), "cs0")
+    S.wait_ge(T.sem.dx0, 16 * len(pieces))
+    done(S.activation(T.cwin[:].indirect(T.du[:, NA // 16:64]), T.xx[:, NA:HE], F.Silu), "cs0")
     wait(S, "cs0")
     S.wait_ge(T.sem.dx1, 32)
     done(S.activation(T.cwin[:].indirect(T.du[:, 64:128]), T.xx[:, HE:NE], F.Silu), "cs")
     wait(S, "cs")
-    done(S.activation(T.cb[:], T.cwin[:, 0:CC], F.Copy), "cb")
-    wait(S, "hm")
-    done(S.activation(T.hm[:], T.psh[:], F.Copy), "hmv")
-    wait(S, "pu", "d1", ("tails", 3), "n1")
-    done(S.activation(T.rr[:], T.d1[:].indirect(T.pu[:, 0:32]), F.Identity, scale=T.n1[:]), "rr")
+    done(S.activation(T.cb[:], T.cwin[:, 0:CC], F.Identity, bias=SH + PF, scale=-1.0), "cb")
+    wait(S, "tr")
+    done(S.activation(T.tf[:], T.pst[:, 0:128], F.Copy), "tf")
+    wait(S, "pw")
+    done(S.activation(T.puf[:], T.psw[:, 0:32], F.Copy), "puf")
+    wait(S, "pq")
+    done(S.activation(T.icf[:], T.psi[:, 0:32], F.Copy), "icf")
+    wait(S, "pu", "b1", ("tails", 2))
+    done(S.activation(T.kk[:, HC:CC], T.b1[:].indirect(T.pu[:, HC // 16:CC // 16]), F.Sign, bias=0.5), "kk")
+    wait(S, "n1")
+    done(S.activation(T.rr[:, HC:CC], T.b1[:].indirect(T.pu[:, HC // 16:CC // 16]), F.Identity, scale=T.n1[:]), "rr")
+    wait(S, "ic")
+    S.wait_ge(T.sem.dnp, 16 * 9)
+    done(S.activation(T.cw[:], T.xx[:].indirect(T.ic[:, 0:32]), F.Copy), "cw")
 
-    wait(P, "ownf", "idf")
-    done(P.transpose(T.psd[:, 0:128], T.ownf[:], T.idf[:]), "tr")
-    for c, (ps, e, e2) in enumerate(((T.psf0, "fa", "ga"), (T.psf1, "fb", "gb"))):
-        wait(P, ("ww", 16), (e2, 2))
+    def turn(ps, w, z, src, lo, hi, start, stop):
+        m = None
         for s in range(16):
-            m = P.matmul(ps[:, 0:64], T.ww[:, 128 * s:128 * s + 128], T.gat[:, HE * c + s:HE * c + HE:16], s == 0, s == 15)
-        done(m, e)
-    wait(P, "tri", "upp", ("vb", 2), ("vz", 2), "tf")
+            m = P.matmul(ps[:, 0:w], z[:, 15 - s:143 - s], src[:, lo + s:hi:16], start and s == 0, stop and s == 15)
+        return m
+
+    wait(P, "za")
+    for c, (ps, e, e2) in enumerate(((T.psf0, "fa", "ga"), (T.psf1, "fb", "gb"))):
+        wait(P, (e2, 2))
+        done(turn(ps, 64, T.za, T.gat, HE * c, HE * c + HE, True, True), e)
+    wait(P, "tri", "upp", ("vb", 2), ("vz", 2))
     P.matmul(T.psd[:, 0:128], T.tri[:], T.vb[:, 1:129], True, False)
     done(P.matmul(T.psd[:, 0:128], T.upp[:], T.vb[:, 0:128], False, True), "dl")
-    wait(P, ("kab", 3))
-    done(P.matmul(T.psh[:], T.ka[0:16, :], T.kb3[0:16, :], True, True), "hm")
-    done(P.matmul(T.psr[:], T.ka[0:16, :], T.kb2[0:16, :], True, True), "rh")
-    wait(P, "cb", "iv")
-    for s in range(16):
-        m = P.matmul(T.psw[:, 0:32], T.ww[:, 128 * s:128 * s + 128], T.cb[:, s:CC:16], s == 0, s == 15)
-    done(m, "pw")
-    wait(P, "vb2", "ds")
+    wait(P, "csa", ("iv", 2))
+    turn(T.psw, 32, T.za, T.ca, 0, CC, True, False)
+    wait(P, "zi")
+    turn(T.psi, 32, T.zi, T.ca, 0, CC, True, False)
+    wait(P, "ownf", "idf")
+    done(P.transpose(T.pst[:, 0:128], T.ownf[:], T.idf[:]), "tr")
+    wait(P, "cb")
+    done(turn(T.psw, 32, T.za, T.cb, 0, CC, False, True), "pw")
+    done(turn(T.psi, 32, T.zi, T.cb, 0, CC, False, True), "pq")
+    wait(P, "zk", ("kk", 2))
+    done(turn(T.psk, 32, T.zk, T.kk, 0, CC, True, True), "pk")
+    wait(P, "vb2", "du")
     P.matmul(T.psd[:, 0:32], T.tri[:], T.vb2[:, 1:33], True, False)
     done(P.matmul(T.psd[:, 0:32], T.upp[:], T.vb2[:, 0:32], False, True), "dl2")
 
     done(V.tensor_copy(T.pmf[:], T.pm[:]), "pmf")
-    done(V.tensor_scalar(T.c1[:], T.pm[:], 1.0, None, A.is_equal), "c1")
     wait(V, "ii", "pmf", "c1")
     done(V.tensor_scalar(T.i512[:], T.ii[:], T.pmf[:], None, A.add), "i512")
     done(V.tensor_scalar(T.i128[:], T.ii[:, 0:32], T.pmf[:], float(ZZ - CC), A.add, A.add), "i128")
     done(V.tensor_scalar(T.n1[:], T.c1[:], -1.0, 1.0, A.mult, A.add), "n1")
-    for c, (ps, e, e2) in enumerate(((T.psf0, "fa", "fva"), (T.psf1, "fb", "fvb"))):
+    done(V.tensor_copy(T.ownf[:], T.owni[:]), "ownf")
+    wait(V, "i512")
+    for c, (ps, e) in enumerate(((T.psf0, "fa"), (T.psf1, "fb"))):
         wait(V, e)
-        done(V.tensor_copy(T.fu[:, 64 * c:64 * c + 64], ps[:, 0:64]), e2)
         done(V.tensor_scalar(T.vb[:, 1 + 64 * c:65 + 64 * c], ps[:, 0:64], float(NE), None, A.is_lt), "vb")
+        done(V.tensor_scalar(T.fu[:, 64 * c:64 * c + 64], ps[:, 0:64], float(NONE), None, A.min), "fu")
         done(V.tensor_scalar(T.psw[:, 64 * c:64 * c + 64], ps[:, 0:64], float(NE), None, A.is_ge), "nv")
-    wait(V, ("nv", 2), "i512")
-    done(V.tensor_tensor(T.iv[:], T.psw[:, 0:128], T.i512[:], A.mult), "iv")
+        wait(V, ("nv", c + 1))
+        done(V.tensor_tensor(T.iv[:, 64 * c:64 * c + 64], T.psw[:, 64 * c:64 * c + 64], T.i512[:, 64 * c:64 * c + 64], A.mult), "iv")
     wait(V, "dl", "zf")
     done(V.tensor_tensor_scan(T.psd[:, 128:256], T.psd[:, 0:128], T.zf[:], 0.0, A.add, A.add), "xs")
-    wait(V, "xs", "iv")
+    wait(V, "xs", ("iv", 2))
     done(V.tensor_tensor(T.ds[:], T.psd[:, 128:256], T.iv[:], A.max), "ds")
     wait(V, "ds")
     done(V.tensor_copy(T.du[:], T.ds[:]), "du")
-    V.wait_ge(T.sem.rep4, 256)
-    V.wait_ge(T.sem.rep3, 256)
-    wait(V, "w4t")
-    for h, rs in enumerate(("fa3a", "fa3b")):
-        V.wait_ge(T.sem[rs], NEG)
-        done(V.tensor_tensor(T.d3[:, HE * h:HE * h + HE], T.w4[:].indirect(T.fl3[:, 64 * h:64 * h + 64]), T.p3[:, HE * h:HE * h + HE], A.add), "d3")
+    wait(V, "du", "cap", ("ipat", ni))
+    done(V.tensor_tensor(T.ca[:].indirect(T.du[:, 0:NA // 16]), T.gat[:, 0:NA], T.ipat[:], A.add), "csa")
+    V.wait_ge(T.sem.dr3, 16)
+    V.wait_ge(T.sem.dr2, 16)
+    wait(V, "w3t")
     V.wait_ge(T.sem.fa2, NEG)
-    V.wait_ge(T.sem.rep2, 256)
-    wait(V, ("tails", 3), ("d3", 2))
-    done(V.tensor_tensor(T.d2[:, 0:NE], T.d3[:].indirect(T.fl2[:, 0:128]), T.p2[:], A.add), "d2")
+    done(V.tensor_tensor(T.b2[:, 0:NE], T.w3[:].indirect(T.fl2[:, 0:128]), T.val[:], A.add), "b2")
     V.wait_ge(T.sem.fa1, NEG)
-    V.wait_ge(T.sem.rep1, 256)
-    wait(V, "d2")
-    done(V.tensor_tensor(T.d1[:, 0:NE], T.d2[:].indirect(T.fl1[:, 0:128]), T.p1[:], A.add), "d1")
-    wait(V, "pw")
-    done(V.tensor_scalar(T.pu[:], T.psw[:, 0:32], -272.0, None, A.add), "pu")
-    wait(V, "pu", "d1", "hmv")
-    done(V.tensor_tensor(T.s1[:], T.d1[:].indirect(T.pu[:, 0:32]), T.hm[:], A.add), "s1")
-    wait(V, "s1", "rh")
-    done(V.tensor_tensor_scan(T.sw[:], T.psr[:], T.s1[:], 0.0, A.max, A.min), "sw")
-    wait(V, "sw")
-    done(V.tensor_scalar(T.vb2[:, 1:33], T.sw[:, 15:CC:16], 0.0, None, A.is_ge), "vb2")
-    done(V.tensor_scalar(T.nv2[:], T.sw[:, 15:CC:16], 0.0, None, A.is_lt), "nv2")
+    V.wait_ge(T.sem.dr1, 16)
+    wait(V, ("tails", 2), "b2")
+    done(V.tensor_tensor(T.b1[:, 0:NE], T.b2[:].indirect(T.fl1[:, 0:128]), T.p1[:], A.add), "b1")
+    V.wait_ge(T.sem.qa1, NEG)
+    done(V.tensor_scalar(T.pu[:], T.pur[:], ROUND, ROUND, A.add, A.subtract), "pu")
+    wait(V, "pu", "b1")
+    done(V.tensor_scalar(T.kk[:, 0:HC], T.b1[:].indirect(T.pu[:, 0:HC // 16]), 0.0, None, A.is_ge), "kk")
+    wait(V, "n1")
+    done(V.tensor_scalar(T.rr[:, 0:HC], T.b1[:].indirect(T.pu[:, 0:HC // 16]), T.n1[:], None, A.mult), "rr")
+    V.wait_ge(T.sem.qa2, NEG)
+    done(V.tensor_scalar(T.ic[:], T.icr[:], ROUND, ROUND, A.add, A.subtract), "ic")
+    wait(V, "pk")
+    done(V.tensor_scalar(T.vb2[:, 1:33], T.psk[:, 0:32], 0.5, None, A.is_ge), "vb2")
+    done(V.tensor_scalar(T.nv2[:], T.psk[:, 0:32], 0.5, None, A.is_lt), "nv2")
     wait(V, "nv2", "i128")
     done(V.tensor_tensor(T.iv2[:], T.nv2[:], T.i128[:], A.mult), "iv2")
-    wait(V, "opre")
-    done(V.tensor_scalar(T.owin[:, 0:ZZ], T.owin[:, 0:ZZ], T.c1[:], None, A.subtract), "opre2")
     wait(V, "dl2")
     done(V.tensor_tensor_scan(T.xs2[:], T.psd[:, 0:32], T.zf[:, 0:32], 0.0, A.add, A.add), "xs2")
     wait(V, "xs2", "iv2")
     done(V.tensor_tensor(T.ds2[:], T.xs2[:], T.iv2[:], A.max), "ds2")
     wait(V, "ds2")
     done(V.tensor_copy(T.du2[:], T.ds2[:]), "du2")
-    wait(V, "du2", "rr", "cs", "opre2")
-    done(V.tensor_tensor(T.owin[:].indirect(T.du2[:, 0:32]), T.rr[:], T.cwin[:, 0:CC], A.add), "osc")
-    wait(V, "osc")
-    done(V.tensor_scalar(T.of[:], T.owin[:, 0:ZZ], ROUND, ROUND + 32.0, A.add, A.subtract), "of")
+    wait(V, "du2", ("rr", 2), "cw", "opre")
+    done(V.tensor_tensor(T.owin[:].indirect(T.du2[:, 0:32]), T.rr[:], T.cw[:], A.add), "osc")
 
-    wait(Y, "of")
-    Y.dma_start(T.yk[:], T.of[1:128:16, :]).then_inc(T.sem.out1, 16)
+    wait(Y, "osc")
+    Y.dma_start(T.yk[:], T.owin[1:128:16, 0:ZZ]).then_inc(T.sem.out1, 16)
     Y.wait_ge(T.sem.out1, 16)
-    wait(S, "of")
-    S.dma_start(T.ys[:], T.of[2:128:16, :]).then_inc(T.sem.out2, 16)
+    wait(S, "osc")
+    S.dma_start(T.ys[:], T.owin[2:128:16, 0:ZZ]).then_inc(T.sem.out2, 16)
     S.wait_ge(T.sem.out2, 16)
-    for s in ("osent", "psent", "fs3", "fs2", "fs1"):
-        g.wait_ge(T.sem[s], 2 * NEG if s == "fs3" else NEG)
+    for s in ("nsent", "xsent", "fs2", "fs1", "qs1", "qs2"):
+        g.wait_ge(T.sem[s], 2 * NEG if s == "xsent" else NEG)

from concourse.bass import DstId, RemoteDMATransfer
from concourse.mybir import dt, AluOpType, AxisListType, ActivationFunctionType

A = AluOpType
F = ActivationFunctionType
NV = 16384
NE = 2048
HE = NE // 2
QE = NE // 4
CH = 256
BIG = 8192.0
PF = 8.0
NONE = 8 * CH + 8
DW = NONE + 8
CC = 512
HC = CC // 2
ZZ = 128
SH = 16.0
NA = 576
NVEC = 6656
NDMA = 4096
NGP = 1024
FW = 1024
ROUND = 8388608.0


def _bufs():
    d = {}
    for where, typ, items in (
            ("sbuf", "int32", "owni:128 nxti:128 ptsi:128 pi:1 pm:1"),
            ("sbuf", "uint16", "ou:128 nu:128 nr:128 fu:128 fl1:128 fl2:128 du:128 pu:32 ic:32 du2:32"),
            ("sbuf", "bfloat16", "ptsb:128 xl1:128 p1:2048 w3:%d tab:16384 val:2048 gat:2048 lo:256 ipat:%d ca:%d cb:512 kk:512 ones:128"
                                 " bd0:128 bd:128 tri:128 upp:128 za:144 zi:144 zk:144 vb:129 vb2:33" % (DW, NA, CC + NA)),
            ("sbuf", "float32", "b2:%d b1:%d xx:%d ownf:128 ptf:128 tf:128 ilo:512 cwin:2560 rr:512 cw:512 owin:640"
                                " zf:128 pmf:1 c0:1 c1:1 c2:1 c3:1 c1n:1 c2n:1 wc:1 wi:1 n1:1 i8:8 bcol:8 bco1:8 bcn:8 idf:128 onef:128"
                                " ii:128 i512:128 i128:32 iv:128 ds:128 nv2:32 iv2:32 xs2:32 ds2:32 puf:32 icf:32 pur:32 icr:32" % (DW, DW, DW)),
            ("dram", "bfloat16", "xo:128 xl2:128 xl3:128 xl4:128"),
            ("psum", "float32", "psf0:512 psf1:512 psd:512 psw:512 psi:512 psk:512 pst:512")):
        for it in items.split():
            name, w = it.split(":")
            d[name] = (where, [128, int(w)], typ)
    return d


SCRATCH = _bufs()
EV = """ones tabg tab0 tabv tabs pi pm pmf c0 c1 c2 c3 cn n1 wc lo ilo i8 bcol bco1 bcn val onef bd0 bd tri upp idf zf z0 za zi zk ipat cap xxi
ii i512 i128 w3t tails cpre vz opre ownf ptf tr tf ptsb nu ou scat ga gb fa fb fu vb nv iv dl xs ds du
xc0 xc1 csa cs0 cs cb pw pq puf icf pu ic kk pk b2 b1 rr cw vb2 nv2 iv2 dl2 xs2 ds2 du2 osc""".split()
SEMAPHORES = ["e_" + e for e in EV] + ["ldo", "ldn", "ldp", "dfl", "dvl", "din", "dxo", "dnp", "dx0", "dx1", "dr1", "dr2", "dr3", "dpt", "narr", "nsent",
                                       "xa1", "xa2", "xa3", "xa4", "xsent", "fa1", "fa2", "fs1", "fs2", "qa1", "qa2", "qs1", "qs2", "out1", "out2"]


def rank_program(g, core, T, topo):
    rank = T.rank_of(core)
    if rank is None:
        return
    n = len(T.cores)
    V, S, P, Y = g.vector, g.scalar, g.tensor, g.sync
    back = [T.cores[(rank - k) % n] for k in range(n)]
    after = T.cores[(rank + 1) % n]

    def sem(e):
        return T.sem["e_" + e]

    def done(ins, e):
        ins.then_inc(sem(e), 1)

    def wait(q, *es):
        for e in es:
            if isinstance(e, tuple):
                q.wait_ge(sem(e[0]), e[1])
            else:
                q.wait_ge(sem(e), 1)

    def const(buf, v, e):
        done(g.iota(buf, [[0, buf.shape[1]]], int(v), 0, allow_small_or_imprecise_dtypes=True), e)

    es = set(topo.engines(core, after))
    for k in range(1, n - 1):
        es &= set(topo.engines(core, back[k]))
    E = sorted(es)[0:8]
    M = sum(1 << e for e in E)
    NEG = len(E)

    def send(dst_ap, src_ap, dst, rs, ls):
        rid, pid = topo.addr(dst)[:2]
        g.remote_dma(dst_ap, src_ap, T.sem[rs], T.sem[ls], pid, rid, M)

    def send_x(k1, k2):
        tr = []
        for k, half in ((k1, E[:NEG // 2]), (k2, E[NEG // 2:])):
            rid, pid = topo.addr(back[k])[:2]
            tr.append(RemoteDMATransfer(dst_ids=[DstId(rid=rid, pnc=pid)], dma_engine_mask=sum(1 << e for e in half), remote_sem=T.sem["xa%d" % k],
                                        srcs=[T.xo[:]], dsts=[T["xl%d" % k][:]]))
        g.remote_dma_fused(tr, local_sem=T.sem.xsent)

    Y.dma_start(T.owni[:], T.own[:]).then_inc(T.sem.ldo, 16)
    S.dma_start(T.nxti[:], T.nxt[:]).then_inc(T.sem.ldn, 16)
    Y.dma_start(T.ptsi[:], T.pts[:]).then_inc(T.sem.ldp, 16)

    done(g.iota(T.pi[:], [[0, 1]], 0, 1), "pi")
    done(g.iota(T.i8[:], [[1, 8]], 0, 0, allow_small_or_imprecise_dtypes=True), "i8")
    done(g.iota(T.lo[:], [[1, CH]], 0, 0, allow_small_or_imprecise_dtypes=True), "lo")
    const(T.tab[:, NVEC + NDMA:NVEC + NDMA + NGP], -BIG, "tabg")
    wait(g, "nu")
    send(T.nr[:], T.nu[:], after, "narr", "nsent")
    const(T.ones[:], 1, "ones")
    wait(g, "ones")
    done(g.affine_select(T.bd0[:], T.ones[:], [[-16, 8], [0, 16]], A.is_ge, 0.0, 0, 1), "bd0")
    wait(g, "bd0")
    done(g.affine_select(T.bd[:], T.bd0[:], [[16, 8], [0, 16]], A.is_ge, 0.0, 15, -1), "bd")
    const(T.za[:], 0, "z0")
    wait(g, "bd")
    done(g.affine_select(T.tri[:], T.bd[:], [[1, 128]], A.is_gt, 0.0, 0, -1), "tri")
    done(g.affine_select(T.upp[:], T.bd[:], [[-1, 128]], A.is_ge, 0.0, 0, 1), "upp")
    done(g.iota(T.ii[:], [[16, 128]], CC, 0, allow_small_or_imprecise_dtypes=True), "ii")
    const(T.zf[:], 0, "zf")
    const(T.vb[:, 0:1], 0, "vz")
    const(T.vb2[:, 0:1], 0, "vz")
    done(g.iota(T.ilo[0:8, :], [[0, QE // CH], [1, CH]], int(SH), 0, allow_small_or_imprecise_dtypes=True), "ilo")
    wait(g, "za")
    const(T.zi[:], 0, "z0")
    const(T.zk[:], 0, "z0")
    const(T.w3[:, NE:DW], -BIG, "w3t")
    g.wait_ge(T.sem.dxo, 16)
    send_x(4, 3)
    wait(g, ("fu", 2))
    send(T.fl2[:], T.fu[:], back[3], "fa2", "fs2")
    send(T.fl1[:], T.fu[:], back[2], "fa1", "fs1")
    send_x(2, 1)
    for b in ("b2", "b1"):
        const(T[b][:, NE:DW], -BIG, "tails")
    const(T.onef[:], 1, "onef")
    wait(g, "onef")
    done(g.affine_select(T.idf[:], T.onef[:], [[-1, 128]], A.is_equal, 0.0, 0, 1), "idf")
    const(T.xx[:, 0:NA], 0, "xxi")
    const(T.xx[:, NE:DW], 0, "xxi")
    wait(g, "ptf")
    g.wait_ge(T.sem.xa1, NEG // 2)
    g.dma_start(T.ptf[:], T.xl1[:], accum_op=A.add).then_inc(T.sem.dpt, 16)
    wait(g, "puf")
    send(T.pur[:], T.puf[:], back[1], "qa1", "qs1")
    wait(g, "icf")
    send(T.icr[:], T.icf[:], back[1], "qa2", "qs2")

    wait(Y, "tab0")
    for a in range(NVEC, NVEC + NDMA, FW):
        Y.dma_start(T.tab[:, a:a + FW], T.tab[:, 0:FW]).then_inc(T.sem.dfl, 16)
    wait(Y, "ptsb", ("val", 8))
    Y.dma_start(T.val[4:128:16, :], T.ptsb[:]).then_inc(T.sem.dvl, 16)
    Y.wait_ge(T.sem.dvl, 16)
    Y.dma_start(T.w3[:, 0:NE], T.val[:]).then_inc(T.sem.din, 16)
    Y.dma_start(T.p1[:], T.val[:]).then_inc(T.sem.din, 16)
    wait(Y, ("ga", 2), ("gb", 2))
    Y.dma_start(T.xo[:], T.gat[4:128:16, :]).then_inc(T.sem.dxo, 16)
    wait(Y, "ilo")
    cuts0 = [NA] + list(range(CH * (NA // CH) + CH, HE + 1, CH))
    pieces = ([(NA, QE)] if NA < QE else []) + [(max(NA, QE), HE)]
    for h, cuts, nx in ((0, pieces, len(cuts0) - 1), (1, [(HE, HE + QE), (HE + QE, NE)], HE // CH)):
        wait(Y, ("xc%d" % h, nx))
        for a, b in cuts:
            Y.dma_start(T.xx[2:128:16, a:b], T.ilo[0:8, a % CH:a % CH + b - a]).then_inc(T.sem["dx%d" % h], 16)
    Y.wait_ge(T.sem.din, 32)
    wait(Y, "scat", "cpre", "cap", "opre")
    Y.wait_ge(T.sem.xa4, NEG // 2)
    Y.dma_start(T.w3[2:128:16, 0:NE], T.xl4[:]).then_inc(T.sem.dr3, 16)
    Y.wait_ge(T.sem.xa3, NEG // 2)
    Y.dma_start(T.val[2:128:16, :], T.xl3[:]).then_inc(T.sem.dr2, 16)
    Y.wait_ge(T.sem.xa2, NEG // 2)
    Y.dma_start(T.p1[2:128:16, :], T.xl2[:]).then_inc(T.sem.dr1, 16)
    wait(Y, "cs", ("xxi", 2), "tf")
    for h in range(8):
        Y.dma_start(T.xx[16 * h + 1:16 * h + 2, 0:NE], T.tf[:, 16 * h:16 * h + 16]).then_inc(T.sem.dnp, 16)
    Y.wait_ge(T.sem.dpt, 16)
    Y.dma_start(T.xx[2:128:16, 0:NE], T.ptf[:]).then_inc(T.sem.dnp, 16)

    done(V.memset(T.tab[:, 0:FW], -BIG), "tab0")
    wait(V, "pi")
    done(V.tensor_scalar(T.pm[:], T.pi[:], 15, None, A.bitwise_and), "pm")
    wait(V, "pm")
    for k in (0, 3):
        done(V.tensor_scalar(T["c%d" % k][:], T.pm[:], float(k), -1.0, A.is_equal, A.mult), "c%d" % k)
    for k in (1, 2):
        done(V.tensor_scalar(T["c%d" % k][:], T.pm[:], float(k), None, A.is_equal), "c%d" % k)
    wait(V, "i8", "c0")
    done(V.tensor_scalar(T.bcol[:], T.i8[:], T.c0[:], None, A.mult), "bcol")
    wait(V, "lo", "c3", "bcol")
    for a in range(8):
        if a == 4:
            V.wait_ge(T.sem.ldn, 16)
            done(V.tensor_copy(T.nu[:], T.nxti[:]), "nu")
        done(V.tensor_scalar(T.val[:, CH * a:CH * a + CH], T.lo[:], T.c3[:], T.bcol[:, a:a + 1], A.mult, A.add), "val")
    V.wait_ge(T.sem.ldp, 16)
    done(V.tensor_copy(T.ptsb[:], T.ptsi[:]), "ptsb")
    V.wait_ge(T.sem.ldo, 16)
    done(V.tensor_copy(T.ou[:], T.owni[:]), "ou")
    done(V.memset(T.tab[:, FW:NVEC], -BIG), "tabv")
    scuts = list(range(NVEC + NDMA + NGP, NV, FW)) + [NV]
    wait(V, "ou", "tabv", "tabg", ("tabs", len(scuts) - 1), ("val", 8), "tab0")
    V.wait_ge(T.sem.dvl, 16)
    V.wait_ge(T.sem.dfl, 16 * (NDMA // FW))
    done(V.tensor_copy(T.tab[:].indirect(T.ou[:, 0:128]), T.val[:]), "scat")
    wait(V, "scat")
    V.wait_ge(T.sem.narr, NEG)
    done(V.tensor_copy(T.gat[:, 0:512], T.tab[:].indirect(T.nr[:, 0:32])), "ga")
    done(V.tensor_copy(T.gat[:, 1024:1536], T.tab[:].indirect(T.nr[:, 64:96])), "gb")

    wait(S, "tab0")
    for a, b in zip(scuts, scuts[1:]):
        done(S.activation(T.tab[:, a:b], T.tab[:, 0:b - a], F.Copy), "tabs")
    wait(S, "c0", "c1", "c2", "c3", "i8")
    done(S.activation(T.wc[:], T.c0[:], F.Identity, bias=T.c3[:], scale=float(CH)), "wc")
    done(S.activation(T.c1n[:], T.c1[:], F.Copy, scale=-1.0), "cn")
    done(S.activation(T.c2n[:], T.c2[:], F.Copy, scale=-1.0), "cn")
    done(S.activation(T.bco1[:], T.i8[:], F.Identity, bias=SH, scale=T.c1[:]), "bco1")
    wait(S, ("cn", 2))
    done(S.activation(T.wi[:], T.c1n[:], F.Identity, bias=T.c2n[:], scale=float(CH)), "wc")
    done(S.activation(T.bcn[:], T.i8[:], F.Copy, scale=T.c1n[:]), "bcn")
    wait(S, "lo", "bcn")
    ni = 0
    for a in range(0, NA, CH):
        b = min(a + CH, NA)
        done(S.activation(T.ipat[:, a:b], T.lo[:, 0:b - a], F.Identity, bias=T.bcn[:, a // CH:a // CH + 1], scale=T.c2n[:]), "ipat")
        ni += 1
    wait(S, ("val", 8))
    S.wait_ge(T.sem.dvl, 16)
    done(S.activation(T.cwin[:, 0:CC], T.val[:, 0:CC], F.Silu, bias=SH + PF, scale=0.0), "cpre")
    done(S.activation(T.ca[:, 0:CC], T.val[:, 0:CC], F.Identity, bias=-PF, scale=0.0), "cap")
    wait(S, ("wc", 2), "bd", "z0")
    done(S.activation(T.za[:, 15:143:16], T.bd[:, 0:128:16], F.Copy, scale=T.wc[:]), "za")
    done(S.activation(T.owin[:, 0:ZZ], T.val[:, 0:ZZ], F.Identity, bias=T.c1n[:], scale=0.0), "opre")
    wait(S, "ptsb")
    done(S.activation(T.ptf[:], T.ptsb[:], F.Copy), "ptf")
    wait(S, "scat")
    S.wait_ge(T.sem.narr, NEG)
    done(S.activation(T.gat[:, 512:1024], T.tab[:].indirect(T.nr[:, 32:64]), F.Copy), "ga")
    done(S.activation(T.gat[:, 1536:2048], T.tab[:].indirect(T.nr[:, 96:128]), F.Copy), "gb")
    wait(S, ("ga", 2), "bco1")
    for h, cuts in ((0, cuts0), (1, list(range(HE, NE + 1, CH)))):
        if h:
            wait(S, ("gb", 2))
        for a, b in zip(cuts, cuts[1:]):
            done(S.activation(T.xx[:, a:b], T.gat[:, a:b], F.Identity, bias=T.bco1[:, a // CH:a // CH + 1], scale=-1.0), "xc%d" % h)
    wait(S, ("z0", 3))
    done(S.activation(T.zi[:, 15:143:16], T.bd[:, 0:128:16], F.Copy, scale=T.wi[:]), "zi")
    done(S.activation(T.zk[:, 15:143:16], T.bd[:, 0:128:16], F.Copy, scale=T.c2[:]), "zk")
    wait(S, "du", "cpre")
    S.wait_ge(T.sem.dx0, 16 * len(pieces))
    done(S.activation(T.cwin[:].indirect(T.du[:, NA // 16:64]), T.xx[:, NA:HE], F.Silu), "cs0")
    wait(S, "cs0")
    S.wait_ge(T.sem.dx1, 32)
    done(S.activation(T.cwin[:].indirect(T.du[:, 64:128]), T.xx[:, HE:NE], F.Silu), "cs")
    wait(S, "cs")
    done(S.activation(T.cb[:], T.cwin[:, 0:CC], F.Identity, bias=SH + PF, scale=-1.0), "cb")
    wait(S, "tr")
    done(S.activation(T.tf[:], T.pst[:, 0:128], F.Copy), "tf")
    wait(S, "pw")
    done(S.activation(T.puf[:], T.psw[:, 0:32], F.Copy), "puf")
    wait(S, "pq")
    done(S.activation(T.icf[:], T.psi[:, 0:32], F.Copy), "icf")
    wait(S, "pu", "b1", ("tails", 2))
    done(S.activation(T.kk[:, HC:CC], T.b1[:].indirect(T.pu[:, HC // 16:CC // 16]), F.Sign, bias=0.5), "kk")
    wait(S, "n1")
    done(S.activation(T.rr[:, HC:CC], T.b1[:].indirect(T.pu[:, HC // 16:CC // 16]), F.Identity, scale=T.n1[:]), "rr")
    wait(S, "ic")
    S.wait_ge(T.sem.dnp, 16 * 9)
    done(S.activation(T.cw[:], T.xx[:].indirect(T.ic[:, 0:32]), F.Copy), "cw")

    def turn(ps, w, z, src, lo, hi, start, stop):
        m = None
        for s in range(16):
            m = P.matmul(ps[:, 0:w], z[:, 15 - s:143 - s], src[:, lo + s:hi:16], start and s == 0, stop and s == 15)
        return m

    wait(P, "za")
    for c, (ps, e, e2) in enumerate(((T.psf0, "fa", "ga"), (T.psf1, "fb", "gb"))):
        wait(P, (e2, 2))
        done(turn(ps, 64, T.za, T.gat, HE * c, HE * c + HE, True, True), e)
    wait(P, "tri", "upp", ("vb", 2), ("vz", 2))
    P.matmul(T.psd[:, 0:128], T.tri[:], T.vb[:, 1:129], True, False)
    done(P.matmul(T.psd[:, 0:128], T.upp[:], T.vb[:, 0:128], False, True), "dl")
    wait(P, "csa", ("iv", 2))
    turn(T.psw, 32, T.za, T.ca, 0, CC, True, False)
    wait(P, "zi")
    turn(T.psi, 32, T.zi, T.ca, 0, CC, True, False)
    wait(P, "ownf", "idf")
    done(P.transpose(T.pst[:, 0:128], T.ownf[:], T.idf[:]), "tr")
    wait(P, "cb")
    done(turn(T.psw, 32, T.za, T.cb, 0, CC, False, True), "pw")
    done(turn(T.psi, 32, T.zi, T.cb, 0, CC, False, True), "pq")
    wait(P, "zk", ("kk", 2))
    done(turn(T.psk, 32, T.zk, T.kk, 0, CC, True, True), "pk")
    wait(P, "vb2", "du")
    P.matmul(T.psd[:, 0:32], T.tri[:], T.vb2[:, 1:33], True, False)
    done(P.matmul(T.psd[:, 0:32], T.upp[:], T.vb2[:, 0:32], False, True), "dl2")

    done(V.tensor_copy(T.pmf[:], T.pm[:]), "pmf")
    wait(V, "ii", "pmf", "c1")
    done(V.tensor_scalar(T.i512[:], T.ii[:], T.pmf[:], None, A.add), "i512")
    done(V.tensor_scalar(T.i128[:], T.ii[:, 0:32], T.pmf[:], float(ZZ - CC), A.add, A.add), "i128")
    done(V.tensor_scalar(T.n1[:], T.c1[:], -1.0, 1.0, A.mult, A.add), "n1")
    done(V.tensor_copy(T.ownf[:], T.owni[:]), "ownf")
    wait(V, "i512")
    for c, (ps, e) in enumerate(((T.psf0, "fa"), (T.psf1, "fb"))):
        wait(V, e)
        done(V.tensor_scalar(T.vb[:, 1 + 64 * c:65 + 64 * c], ps[:, 0:64], float(NE), None, A.is_lt), "vb")
        done(V.tensor_scalar(T.fu[:, 64 * c:64 * c + 64], ps[:, 0:64], float(NONE), None, A.min), "fu")
        done(V.tensor_scalar(T.psw[:, 64 * c:64 * c + 64], ps[:, 0:64], float(NE), None, A.is_ge), "nv")
        wait(V, ("nv", c + 1))
        done(V.tensor_tensor(T.iv[:, 64 * c:64 * c + 64], T.psw[:, 64 * c:64 * c + 64], T.i512[:, 64 * c:64 * c + 64], A.mult), "iv")
    wait(V, "dl", "zf")
    done(V.tensor_tensor_scan(T.psd[:, 128:256], T.psd[:, 0:128], T.zf[:], 0.0, A.add, A.add), "xs")
    wait(V, "xs", ("iv", 2))
    done(V.tensor_tensor(T.ds[:], T.psd[:, 128:256], T.iv[:], A.max), "ds")
    wait(V, "ds")
    done(V.tensor_copy(T.du[:], T.ds[:]), "du")
    wait(V, "du", "cap", ("ipat", ni))
    done(V.tensor_tensor(T.ca[:].indirect(T.du[:, 0:NA // 16]), T.gat[:, 0:NA], T.ipat[:], A.add), "csa")
    V.wait_ge(T.sem.dr3, 16)
    V.wait_ge(T.sem.dr2, 16)
    wait(V, "w3t")
    V.wait_ge(T.sem.fa2, NEG)
    done(V.tensor_tensor(T.b2[:, 0:NE], T.w3[:].indirect(T.fl2[:, 0:128]), T.val[:], A.add), "b2")
    V.wait_ge(T.sem.fa1, NEG)
    V.wait_ge(T.sem.dr1, 16)
    wait(V, ("tails", 2), "b2")
    done(V.tensor_tensor(T.b1[:, 0:NE], T.b2[:].indirect(T.fl1[:, 0:128]), T.p1[:], A.add), "b1")
    V.wait_ge(T.sem.qa1, NEG)
    done(V.tensor_scalar(T.pu[:], T.pur[:], ROUND, ROUND, A.add, A.subtract), "pu")
    wait(V, "pu", "b1")
    done(V.tensor_scalar(T.kk[:, 0:HC], T.b1[:].indirect(T.pu[:, 0:HC // 16]), 0.0, None, A.is_ge), "kk")
    wait(V, "n1")
    done(V.tensor_scalar(T.rr[:, 0:HC], T.b1[:].indirect(T.pu[:, 0:HC // 16]), T.n1[:], None, A.mult), "rr")
    V.wait_ge(T.sem.qa2, NEG)
    done(V.tensor_scalar(T.ic[:], T.icr[:], ROUND, ROUND, A.add, A.subtract), "ic")
    wait(V, "pk")
    done(V.tensor_scalar(T.vb2[:, 1:33], T.psk[:, 0:32], 0.5, None, A.is_ge), "vb2")
    done(V.tensor_scalar(T.nv2[:], T.psk[:, 0:32], 0.5, None, A.is_lt), "nv2")
    wait(V, "nv2", "i128")
    done(V.tensor_tensor(T.iv2[:], T.nv2[:], T.i128[:], A.mult), "iv2")
    wait(V, "dl2")
    done(V.tensor_tensor_scan(T.xs2[:], T.psd[:, 0:32], T.zf[:, 0:32], 0.0, A.add, A.add), "xs2")
    wait(V, "xs2", "iv2")
    done(V.tensor_tensor(T.ds2[:], T.xs2[:], T.iv2[:], A.max), "ds2")
    wait(V, "ds2")
    done(V.tensor_copy(T.du2[:], T.ds2[:]), "du2")
    wait(V, "du2", ("rr", 2), "cw", "opre")
    done(V.tensor_tensor(T.owin[:].indirect(T.du2[:, 0:32]), T.rr[:], T.cw[:], A.add), "osc")

    wait(Y, "osc")
    Y.dma_start(T.yk[:], T.owin[1:128:16, 0:ZZ]).then_inc(T.sem.out1, 16)
    Y.wait_ge(T.sem.out1, 16)
    wait(S, "osc")
    S.dma_start(T.ys[:], T.owin[2:128:16, 0:ZZ]).then_inc(T.sem.out2, 16)
    S.wait_ge(T.sem.out2, 16)
    for s in ("nsent", "xsent", "fs2", "fs1", "qs1", "qs2"):
        g.wait_ge(T.sem[s], 2 * NEG if s == "xsent" else NEG)
